import numpy as np
import ml_dtypes


def mxq(x, axis, fmt="e4m3"):
    dtype, down = {"e4m3": (ml_dtypes.float8_e4m3fn, 7), "e5m2": (ml_dtypes.float8_e5m2, 14)}[fmt]
    v = np.moveaxis(np.asarray(x, np.float32).astype(ml_dtypes.bfloat16).astype(np.float64), axis, -1)
    blocks = v.reshape(v.shape[:-1] + (-1, 32))
    amax = np.abs(blocks).max(-1, keepdims=True)
    byte = np.maximum(np.where(amax > 0, np.frexp(amax)[1] - 1 + 127, 0) - down, 1)
    scale = np.exp2(byte - 127.0)
    codes = (blocks / scale).astype(np.float32).astype(dtype).astype(np.float64)
    return np.moveaxis((codes * scale).reshape(v.shape), -1, axis)


WIDE = False


def mx_kscale(k):
    if not WIDE:
        return np.ones(k)
    levels = np.array([10, -10, 5, -5, 0])
    if k % 512:
        return np.exp2(np.random.permutation(np.resize(levels, k // 32))).repeat(32)
    a = np.empty((k // 512, 16))
    for p in range(k // 512):
        a[p, :8] = np.random.permutation(np.resize(levels, 8))
        for g in range(8):
            far = levels[np.abs(levels - a[p, g]) >= 10]
            a[p, g + 8] = far[np.random.randint(len(far))]
    return np.exp2(a.ravel()).repeat(32)


def f64(x):
    return np.asarray(x).astype(np.float64)


def striped(idx):
    return np.tile(idx.reshape(-1, 16).T, (8, 1)).astype(np.uint16)


def unstriped(offs):
    return offs[:16].T.reshape(-1).astype(np.int64)


E2M1 = np.array([0.0, 0.5, 1.0, 1.5, 2.0, 3.0, 4.0, 6.0, -0.0, -0.5, -1.0, -1.5, -2.0, -3.0, -4.0, -6.0])


def pack_weight(w, fmt):
    k, n = w.shape
    w = f64(np.asarray(w, np.float32).astype(ml_dtypes.bfloat16)).reshape(k // 32, 32, n)
    amax = np.abs(w).max(1)
    if fmt == "e4m3":
        byte = np.frexp(amax)[1] - 1 + 127 - 7
    else:
        mant, ex = np.frexp(amax / 6.0)
        byte = np.where(mant > 0.5, ex, ex - 1) + 127
    byte = np.clip(np.where(amax > 0, byte, 1), 1, 254)
    scaled = (w * np.exp2(127.0 - byte)[:, None, :]).reshape(k, n).astype(np.float32)
    by_word = np.ascontiguousarray(scaled.reshape(k // 512, 128, 4, n).transpose(0, 1, 3, 2))
    if fmt == "e4m3":
        words = by_word.astype(ml_dtypes.float8_e4m3fn).view(np.uint8)
    else:
        c = by_word.astype(ml_dtypes.float4_e2m1fn).view(np.uint8) & 0xF
        words = (c[..., 0::2] | (c[..., 1::2] << 4)).reshape(k // 512, 128, 2 * n)
    return np.ascontiguousarray(words), np.ascontiguousarray(byte.astype(np.uint8).reshape(k // 512, 16, n))


def unpack_weight(words, scales, fmt):
    g, _, n = scales.shape
    words = np.ascontiguousarray(words).reshape(g, 128, n, -1)
    if fmt == "e4m3":
        vals = words.view(ml_dtypes.float8_e4m3fn).astype(np.float64)
    else:
        nib = np.empty((g, 128, n, 4), np.uint8)
        nib[..., 0::2] = words & 0xF
        nib[..., 1::2] = words >> 4
        vals = E2M1[nib]
    vals = vals * np.repeat(np.exp2(scales.astype(np.float64) - 127.0), 8, axis=1)[..., None]
    return vals.transpose(0, 1, 3, 2).reshape(g * 512, n)


def relu(v):
    return np.maximum(v, 0.0)


K, T, E, C, H, N = 1536, 512, 4, 256, 512, 128


def by_expert(wq, xq):
    return np.concatenate([wq[e].T @ xq[:, e * C:(e + 1) * C] for e in range(E)], axis=1)


def setup_inputs():
    n = np.random.standard_normal
    s = mx_kscale(K)
    u = mx_kscale(H)
    first = np.random.permutation(np.repeat(np.arange(E), T // E))
    second = (first + 1 + np.random.permutation(np.repeat(np.arange(E - 1), -(-T // (E - 1)))[:T])) % E
    while np.bincount(second, minlength=E).max() != T // E:
        load = np.bincount(second, minlength=E); hi, lo = int(load.argmax()), int(load.argmin())
        t = np.flatnonzero((second == hi) & (first != lo))[0]; second[t] = lo
    slot_token = np.empty(E * C, np.int64); pos = np.empty((2, T), np.int64); fill = np.zeros(E, np.int64)
    place = np.stack([np.random.permutation(C) for _ in range(E)])
    for r, deal in enumerate((first, second)):
        for t in np.random.permutation(T):
            e = deal[t]; j = e * C + place[e, fill[e]]; fill[e] += 1; slot_token[j] = t; pos[r, t] = j
    g = np.random.uniform(0.2, 0.8, T)
    x = pack_weight(n((K, T)) * s[:, None], "e4m3")
    w = [pack_weight(m, "e2m1") for m in n((E, K, N)) / np.sqrt(K) / s[None, :, None]]
    return {
        "x_words": x[0],
        "x_scales": x[1],
        "w_words": np.stack([m[0] for m in w]),
        "w_scales": np.stack([m[1] for m in w]),
        "wa": (n((E, K, H)) / np.sqrt(K) / s[None, :, None] * u).astype(np.float32),
        "wb": (n((E, H, N)) / np.sqrt(H) / u[None, :, None]).astype(np.float32),
        "gate": np.stack([np.tile(g, (128, 1)), np.tile(1.0 - g, (128, 1))]).astype(np.float32),
        "offs": striped(slot_token),
        "pos1": striped(pos[0]),
        "pos2": striped(pos[1]),
    }


def reference(x_words, x_scales, w_words, w_scales, wa, wb, gate, offs, pos1, pos2):
    w = np.stack([unpack_weight(w_words[e], w_scales[e], "e2m1") for e in range(E)])
    waq = mxq(f64(wa), 1, "e4m3")
    wbq = mxq(f64(wb), 1, "e4m3")
    idx = unstriped(offs)
    xq = unpack_weight(x_words, x_scales, "e4m3")[:, idx]
    h = relu(by_expert(waq, xq))
    y = by_expert(w, xq) + by_expert(wbq, mxq(h, 0, "e4m3"))
    out = sum(f64(gate[r, :1]) * y[:, unstriped(p)] for r, p in enumerate((pos1, pos2)))
    return out

@@ -1,0 +1,256 @@
+from contextlib import ExitStack
+
+import concourse.mybir as mybir
+
+K, T, E, C, H, N = 1536, 512, 4, 256, 512, 128
+FLOPS = 2 * E * C * (K * H + K * N + H * N)
+
+F32 = mybir.dt.float32
+BF16 = mybir.dt.bfloat16
+I32 = mybir.dt.int32
+U32 = mybir.dt.uint32
+U16 = mybir.dt.uint16
+U8 = mybir.dt.uint8
+FP8X4 = mybir.dt.float8_e4m3fn_x4
+FP4X4 = mybir.dt.float4_e2m1fn_x4
+RELU = mybir.ActivationFunctionType.Relu
+ALU = mybir.AluOpType
+
+P = 128
+PACK = 4
+PASSES = K // (P * PACK)
+HALF = 128
+SPLIT = 92
+RAW_SLOTS = 6
+RAW_BYTES = PACK * H * 4
+BF_BYTES = PACK * H * 2
+
+
+def tile_moe_elr_relu_kernel(
+    tc, x_words, x_scales, w_words, w_scales, wa, wb, gate, offs, pos1, pos2, out
+):
+    nc = tc.nc
+    with ExitStack() as ctx:
+        keep = ctx.enter_context(tc.tile_pool(name="keep", bufs=1))
+        ring = ctx.enter_context(tc.tile_pool(name="ring", bufs=4))
+        arena = ctx.enter_context(tc.tile_pool(name="arena", bufs=1))
+        psum = ctx.enter_context(tc.psum_pool(name="psum", bufs=2))
+
+        def kept(shape, dtype, name):
+            return keep.tile(shape, dtype, name=name, align_bytes=64)
+
+        def placed(shape, dtype, name, offset):
+            return arena.tile(shape, dtype, name=name, align_bytes=64, offset=offset)
+
+        def raw_at(i):
+            return (i % RAW_SLOTS) * RAW_BYTES
+
+        def bf_at(i):
+            return RAW_SLOTS * RAW_BYTES + i * BF_BYTES
+
+        offs_sb = keep.tile([P, E * C // 16], U16, name="offs_sb")
+        pos1_sb = keep.tile([P, T // 16], U16, name="pos1_sb")
+        pos2_sb = keep.tile([P, T // 16], U16, name="pos2_sb")
+        xw = [kept([P, T], I32, "xw%d" % s) for s in range(PASSES)]
+        xs = kept([P, T], U8, "xs")
+        xsg = kept([P, E * C], U8, "xsg")
+        xs0 = kept([P, PASSES - 1, E * C], U8, "xs0")
+        ww = kept([P, E * PASSES, 2 * N], U8, "ww")
+        ws = kept([P, E * PASSES, N], U8, "ws")
+        wa_raw = {}
+        wb_raw = [kept([P, PACK, N], F32, "wb_raw%d" % e) for e in range(E)]
+        gate_sb = []
+        y_sb = kept([P, E * C], F32, "y_sb")
+
+        warm = kept([P, 8], F32, "warm")
+        nc.vector.memset(warm[:, 0:1], 0.0)
+        nc.scalar.activation(out=warm[:, 1:2], in_=warm[:, 0:1], func=RELU)
+        nc.vector.memset(xs[:].bitcast(I32), 0)
+
+        def load_xs(q, engine):
+            engine.dma_start(out=xs[32 * q : 32 * q + 4 * PASSES, :].bitcast(I32), in_=x_scales.bitcast(I32)[:, 4 * q : 4 * q + 4, :])
+
+        load_xs(0, nc.scalar)
+        load_xs(1, nc.scalar)
+        nc.vector.memset(ws[:].rearrange("p a n -> p (a n)").bitcast(I32), 0)
+        nc.vector.memset(xs0[:].rearrange("p a n -> p (a n)").bitcast(I32), 0)
+        ws_rows = w_scales.bitcast(I32).rearrange("e s (q r) w -> r q (e s) w", r=4)
+
+        def load_ws(r):
+            nc.sync.dma_start(out=ws[r:P:32, :, :].bitcast(I32), in_=ws_rows[r])
+
+        def load_wa(e, s):
+            wa_raw[e, s] = placed([P, PACK, H], F32, "wa_raw%d_%d" % (e, s), raw_at(e * PASSES + s))
+            nc.sync.dma_start(out=wa_raw[e, s][:], in_=wa[e, 512 * s : 512 * (s + 1), :].rearrange("(p j) c -> p j c", j=PACK))
+
+        def load_wb(e):
+            nc.sync.dma_start(out=wb_raw[e][:], in_=wb[e].rearrange("(p j) c -> p j c", j=PACK))
+
+        def load_xw(s):
+            nc.sync.dma_start(out=xw[s][:], in_=x_words[s].rearrange("p t d -> p (t d)").bitcast(I32))
+
+        nc.sync.dma_start(offs_sb[:], offs)
+        load_xw(0)
+        load_wa(0, 0)
+        load_xw(1)
+        load_xs(2, nc.sync)
+        load_xs(3, nc.sync)
+        load_wa(0, 1)
+        load_xw(2)
+        load_wa(0, 2)
+        nc.sync.dma_start(out=ww[:].bitcast(I32), in_=w_words.bitcast(I32).rearrange("e s p w -> p (e s) w"))
+        load_ws(0)
+        load_wb(0)
+        load_ws(1)
+        load_wa(1, 0)
+
+        xg, grouped, codes, scales, h_ps, y_ps = {}, {}, {}, {}, {}, {}
+
+        def gather(e, s):
+            lst = offs_sb[:, e * (C // 16) : (e + 1) * (C // 16)]
+            if e < 2:
+                xg[e, s] = kept([P, C], U32, "xg%d_%d" % (e, s))
+            else:
+                xg[e, s] = placed([P, C], U32, "xg%d_%d" % (e, s), bf_at(e * PASSES + s - 4))
+            nc.vector.tensor_copy(xg[e, s][:], xw[s][:].bitcast(U32).indirect(lst))
+
+        def gather_scales():
+            for e in range(E):
+                lst = offs_sb[:, e * (C // 16) : (e + 1) * (C // 16)]
+                nc.vector.tensor_copy(xsg[:, e * C : (e + 1) * C], xs[:].indirect(lst))
+            for s in range(1, PASSES):
+                nc.sync.dma_start(out=xs0[0:100, s - 1, :].bitcast(I32), in_=xsg[4 * s : 4 * s + 100, :].bitcast(I32))
+
+        def cast_wa(e, s, split):
+            g = placed([P, PACK * H], BF16, "wa_bf%d_%d" % (e, s), bf_at(e * PASSES + s))
+            grouped[e, s] = g
+            dst = g[:].rearrange("p (t m j) -> p m j t", t=PACK, j=PACK)
+            src = wa_raw[e, s][:].rearrange("p j (m t) -> p m j t", t=PACK)
+            nc.scalar.copy(out=dst[:, :split], in_=src[:, :split])
+            nc.vector.tensor_copy(out=dst[:, split:], in_=src[:, split:])
+
+        def quant_wa(e, s):
+            codes[e, s] = ring.tile([P, H], U32, name="wa_codes", align_bytes=64)
+            scales[e, s] = ring.tile([P, H], U8, name="wa_scales", align_bytes=64)
+            nc.vector.quantize_mx(out=codes[e, s][:].bitcast(FP8X4), scales=scales[e, s][:], in_=grouped[e, s][:])
+
+        def mm_wa(e, s):
+            for u in range(2):
+                if s == 0:
+                    h_ps[e, u] = psum.tile([P, PACK, HALF], F32, name="h_ps%d" % u)
+                cols = slice(u * HALF, (u + 1) * HALF)
+                for t in range(PACK):
+                    m = slice(t * P, (t + 1) * P)
+                    nc.tensor.matmul_mx(
+                        out=h_ps[e, u][:, t, :],
+                        lhsT=codes[e, s][:, m].bitcast(FP8X4), lhsT_scale=scales[e, s][:, m],
+                        rhs=xg[e, s][:, cols].bitcast(FP8X4), rhs_scale=xsg[4 * s :, e * C + u * HALF : e * C + (u + 1) * HALF],
+                        start=(s == 0 and t == 0), stop=(s == PASSES - 1 and t == PACK - 1),
+                    )
+
+        def mm_w(e, s):
+            for u in range(2):
+                if s == 0:
+                    y_ps[e, u] = psum.tile([P, HALF], F32, name="y_ps%d" % u)
+                cols = slice(u * HALF, (u + 1) * HALF)
+                slots = slice(e * C + u * HALF, e * C + (u + 1) * HALF)
+                plane = xsg[:, slots] if s == 0 else xs0[:, s - 1, slots]
+                nc.tensor.matmul_mx(
+                    out=y_ps[e, u][:],
+                    lhsT=ww[:, e * PASSES + s, :].bitcast(FP4X4), lhsT_scale=ws[:, e * PASSES + s, :],
+                    rhs=xg[e, s][:, cols].bitcast(FP8X4), rhs_scale=plane,
+                    start=(s == 0), stop=False,
+                )
+
+        wb_bf, wb_codes, wb_scales, h_bf = {}, {}, {}, {}
+
+        def cast_wb(e):
+            wb_bf[e] = ring.tile([P, PACK * N], BF16, name="wb_bf", align_bytes=64)
+            nc.vector.tensor_copy(
+                out=wb_bf[e][:].rearrange("p (c i j) -> p c j i", i=4, j=PACK),
+                in_=wb_raw[e][:].rearrange("p j (c i) -> p c j i", i=4),
+            )
+
+        def quant_wb(e):
+            wb_codes[e] = ring.tile([P, N], U32, name="wb_codes", align_bytes=64)
+            wb_scales[e] = ring.tile([P, N], U8, name="wb_scales", align_bytes=64)
+            nc.vector.quantize_mx(out=wb_codes[e][:].bitcast(FP8X4), scales=wb_scales[e][:], in_=wb_bf[e][:])
+
+        def relu_h(e, u, on_vector):
+            if e < E - 1:
+                h_bf[e, u] = placed([P, HALF, PACK], BF16, "h_bf%d_%d" % (e, u), raw_at(PASSES * (e + 1)) + u * HALF * PACK * 2)
+            else:
+                h_bf[e, u] = kept([P, HALF, PACK], BF16, "h_bf%d_%d" % (e, u))
+            src = h_ps[e, u][:].rearrange("p t n -> p n t")
+            if on_vector:
+                nc.vector.tensor_scalar_max(out=h_bf[e, u][:], in0=src, scalar1=0.0)
+            else:
+                nc.scalar.activation(out=h_bf[e, u][:], in_=src, func=RELU)
+
+        def second(e, u, on_vector):
+            hc = ring.tile([P, HALF], U32, name="h_codes", align_bytes=64)
+            hs = ring.tile([P, HALF], U8, name="h_scales", align_bytes=64)
+            nc.vector.quantize_mx(out=hc[:].bitcast(FP8X4), scales=hs[:], in_=h_bf[e, u][:].rearrange("p n t -> p (n t)"))
+            nc.tensor.matmul_mx(
+                out=y_ps[e, u][:],
+                lhsT=wb_codes[e][:].bitcast(FP8X4), lhsT_scale=wb_scales[e][:],
+                rhs=hc[:].bitcast(FP8X4), rhs_scale=hs[:],
+                start=False, stop=True,
+            )
+            dst = y_sb[:, e * C + u * HALF : e * C + (u + 1) * HALF]
+            if on_vector:
+                nc.vector.tensor_copy(out=dst, in_=y_ps[e, u][:])
+            else:
+                nc.scalar.copy(out=dst, in_=y_ps[e, u][:])
+
+        steps = [(e, s) for e in range(E) for s in range(PASSES)]
+        last = len(steps) - 1
+        gather(0, 0)
+        cast_wa(0, 0, SPLIT)
+        gather_scales()
+        load_ws(2)
+        load_wa(1, 1)
+        load_ws(3)
+        load_wa(1, 2)
+        load_wb(1)
+        for i, (e, s) in enumerate(steps):
+            if i > 0:
+                gather(e, s)
+            if i < last:
+                cast_wa(steps[i + 1][0], steps[i + 1][1], SPLIT if i + 1 < last else 44)
+            quant_wa(e, s)
+            mm_wa(e, s)
+            if s == 0 and e > 0:
+                second(e - 1, 0, False)
+                second(e - 1, 1, False)
+            if s == PASSES - 1:
+                for s2 in range(PASSES):
+                    mm_w(e, s2)
+                relu_h(e, 0, False)
+                cast_wb(e)
+                relu_h(e, 1, e == E - 1)
+                quant_wb(e)
+            if i + 6 <= last:
+                load_wa(steps[i + 6][0], steps[i + 6][1])
+                if steps[i + 6][1] == PASSES - 1:
+                    load_wb(steps[i + 6][0])
+            if i + 6 == last:
+                nc.sync.dma_start(pos1_sb[:], pos1)
+                nc.sync.dma_start(pos2_sb[:], pos2)
+            if i == 8:
+                for r in range(2):
+                    gate_sb.append(placed([P, T], F32, "gate%d" % r, bf_at(8) + r * T * 4))
+                    nc.sync.dma_start(out=gate_sb[r][:], in_=gate[r])
+        second(E - 1, 0, False)
+        second(E - 1, 1, True)
+
+        for b in range(2):
+            tok = slice(b * (T // 2), (b + 1) * (T // 2))
+            lst = slice(b * (T // 32), (b + 1) * (T // 32))
+            part1 = ring.tile([P, T // 2], F32, name="part1")
+            part2 = ring.tile([P, T // 2], F32, name="part2")
+            res = ring.tile([P, T // 2], F32, name="res")
+            nc.vector.tensor_tensor(part1[:], y_sb[:].indirect(pos1_sb[:, lst]), gate_sb[0][:, tok], ALU.mult)
+            nc.vector.tensor_tensor(part2[:], y_sb[:].indirect(pos2_sb[:, lst]), gate_sb[1][:, tok], ALU.mult)
+            nc.vector.tensor_tensor(res[:], part1[:], part2[:], ALU.add)
+            nc.sync.dma_start(out=out[:, tok], in_=res[:])

@@ -20,7 +20,22 @@ P = 128
 PACK = 4
 PASSES = K // (P * PACK)
 HALF = 128
-SPLIT = 92
+SPLITS = [128,128,128,100,48,84,104,64,64,52,44]
+HEAD = ["wa00","offs","xw0","xs3","xs1","xs2","xw1","wa01","xw2","xs0","wa02","wa10"]
+ACT_HEAD = "w"
+WB_ENG = "SVVS"
+YC_ENG = "SVVVS"
+YC_ORDER = [0,4,1,2,3]
+LATE = ["w01","b0","b3","b1","w3","b2","w2"]
+W_FIRST = [True,True,True,True]
+TAIL = ["c0","w2","h0","c1","q1","c3","q3","q0","w3","h1","w1","c2","m3","m1","w0","q2","m0","m2"]
+POS_AT = 0
+RELU_LAG = [1,0,1]
+LAST_V = 96
+LAST_RELU_V = False
+FREE_G = 8
+G_LAG = 6
+WW_AT = 1
 RAW_SLOTS = 6
 RAW_BYTES = PACK * H * 4
 BF_BYTES = PACK * H * 2
@@ -35,6 +50,7 @@ def tile_moe_elr_relu_kernel(
         ring = ctx.enter_context(tc.tile_pool(name="ring", bufs=4))
         arena = ctx.enter_context(tc.tile_pool(name="arena", bufs=1))
         psum = ctx.enter_context(tc.psum_pool(name="psum", bufs=2))
+        ypsum = ctx.enter_context(tc.psum_pool(name="ypsum", bufs=1))
 
         def kept(shape, dtype, name):
             return keep.tile(shape, dtype, name=name, align_bytes=64)
@@ -55,23 +71,23 @@ def tile_moe_elr_relu_kernel(
         xs = kept([P, T], U8, "xs")
         xsg = kept([P, E * C], U8, "xsg")
         xs0 = kept([P, PASSES - 1, E * C], U8, "xs0")
-        ww = kept([P, E * PASSES, 2 * N], U8, "ww")
         ws = kept([P, E * PASSES, N], U8, "ws")
         wa_raw = {}
-        wb_raw = [kept([P, PACK, N], F32, "wb_raw%d" % e) for e in range(E)]
-        gate_sb = []
+        wb_raw = {}
         y_sb = kept([P, E * C], F32, "y_sb")
 
         warm = kept([P, 8], F32, "warm")
-        nc.vector.memset(warm[:, 0:1], 0.0)
-        nc.scalar.activation(out=warm[:, 1:2], in_=warm[:, 0:1], func=RELU)
         nc.vector.memset(xs[:].bitcast(I32), 0)
+        nc.vector.memset(warm[:, 0:1], 0.0)
 
         def load_xs(q, engine):
             engine.dma_start(out=xs[32 * q : 32 * q + 4 * PASSES, :].bitcast(I32), in_=x_scales.bitcast(I32)[:, 4 * q : 4 * q + 4, :])
 
-        load_xs(0, nc.scalar)
-        load_xs(1, nc.scalar)
+        for item in ACT_HEAD:
+            if item == "w":
+                nc.scalar.activation(out=warm[:, 1:2], in_=warm[:, 0:1], func=RELU)
+            else:
+                load_xs(int(item), nc.scalar)
         nc.vector.memset(ws[:].rearrange("p a n -> p (a n)").bitcast(I32), 0)
         nc.vector.memset(xs0[:].rearrange("p a n -> p (a n)").bitcast(I32), 0)
         ws_rows = w_scales.bitcast(I32).rearrange("e s (q r) w -> r q (e s) w", r=4)
@@ -79,67 +95,88 @@ def tile_moe_elr_relu_kernel(
         def load_ws(r):
             nc.sync.dma_start(out=ws[r:P:32, :, :].bitcast(I32), in_=ws_rows[r])
 
-        def load_wa(e, s):
-            wa_raw[e, s] = placed([P, PACK, H], F32, "wa_raw%d_%d" % (e, s), raw_at(e * PASSES + s))
-            nc.sync.dma_start(out=wa_raw[e, s][:], in_=wa[e, 512 * s : 512 * (s + 1), :].rearrange("(p j) c -> p j c", j=PACK))
+        def load_wa(e, s, pieces=((0, H),)):
+            if (e, s) not in wa_raw:
+                wa_raw[e, s] = placed([P, PACK, H], F32, "wa_raw%d_%d" % (e, s), raw_at(e * PASSES + s))
+            rows = wa[e, 512 * s : 512 * (s + 1), :].rearrange("(p j) c -> p j c", j=PACK)
+            for lo, hi in pieces:
+                nc.sync.dma_start(out=wa_raw[e, s][:, :, lo:hi], in_=rows[:, :, lo:hi])
 
         def load_wb(e):
+            wb_raw[e] = placed([P, PACK, N], F32, "wb_raw%d" % e, bf_at(8) + [x for x in LATE if x[0] == "b"].index("b%d" % e) * PACK * N * 4)
             nc.sync.dma_start(out=wb_raw[e][:], in_=wb[e].rearrange("(p j) c -> p j c", j=PACK))
+
+        ww = {}
+
+        def load_ww(lo, hi, offset):
+            words = placed([P, (hi - lo) * PASSES, 2 * N], U8, "ww%d" % lo, offset)
+            for e in range(lo, hi):
+                ww[e] = words[:, (e - lo) * PASSES : (e - lo + 1) * PASSES, :]
+            nc.sync.dma_start(out=words[:].bitcast(I32), in_=w_words[lo:hi].bitcast(I32).rearrange("e s p w -> p (e s) w"))
 
         def load_xw(s):
             nc.sync.dma_start(out=xw[s][:], in_=x_words[s].rearrange("p t d -> p (t d)").bitcast(I32))
 
-        nc.sync.dma_start(offs_sb[:], offs)
-        load_xw(0)
-        load_wa(0, 0)
-        load_xw(1)
-        load_xs(2, nc.sync)
-        load_xs(3, nc.sync)
-        load_wa(0, 1)
-        load_xw(2)
-        load_wa(0, 2)
-        nc.sync.dma_start(out=ww[:].bitcast(I32), in_=w_words.bitcast(I32).rearrange("e s p w -> p (e s) w"))
-        load_ws(0)
-        load_wb(0)
-        load_ws(1)
-        load_wa(1, 0)
+        for item in HEAD:
+            if item == "offs":
+                nc.sync.dma_start(offs_sb[:], offs)
+            elif item[:2] == "xw":
+                load_xw(int(item[2]))
+            elif item[:2] == "xs":
+                load_xs(int(item[2]), nc.sync)
+            else:
+                load_wa(int(item[2]), int(item[3]))
 
-        xg, grouped, codes, scales, h_ps, y_ps = {}, {}, {}, {}, {}, {}
+        xg, grouped, codes, scales, h_ps = {}, {}, {}, {}, {}
 
         def gather(e, s):
             lst = offs_sb[:, e * (C // 16) : (e + 1) * (C // 16)]
-            if e < 2:
+            if e * PASSES + s < FREE_G:
                 xg[e, s] = kept([P, C], U32, "xg%d_%d" % (e, s))
             else:
-                xg[e, s] = placed([P, C], U32, "xg%d_%d" % (e, s), bf_at(e * PASSES + s - 4))
+                xg[e, s] = placed([P, C], U32, "xg%d_%d" % (e, s), bf_at(e * PASSES + s - G_LAG))
             nc.vector.tensor_copy(xg[e, s][:], xw[s][:].bitcast(U32).indirect(lst))
 
-        def gather_scales():
-            for e in range(E):
-                lst = offs_sb[:, e * (C // 16) : (e + 1) * (C // 16)]
-                nc.vector.tensor_copy(xsg[:, e * C : (e + 1) * C], xs[:].indirect(lst))
+        def gather_scales(e):
+            lst = offs_sb[:, e * (C // 16) : (e + 1) * (C // 16)]
+            nc.vector.tensor_copy(xsg[:, e * C : (e + 1) * C], xs[:].indirect(lst))
+
+        def shift_scales():
             for s in range(1, PASSES):
-                nc.sync.dma_start(out=xs0[0:100, s - 1, :].bitcast(I32), in_=xsg[4 * s : 4 * s + 100, :].bitcast(I32))
+                nc.sync.dma_start(out=xs0[0:112, s - 1, :].bitcast(I32), in_=xsg[4 * s : 4 * s + 112, :].bitcast(I32))
 
         def cast_wa(e, s, split):
             g = placed([P, PACK * H], BF16, "wa_bf%d_%d" % (e, s), bf_at(e * PASSES + s))
             grouped[e, s] = g
             dst = g[:].rearrange("p (t m j) -> p m j t", t=PACK, j=PACK)
             src = wa_raw[e, s][:].rearrange("p j (m t) -> p m j t", t=PACK)
-            nc.scalar.copy(out=dst[:, :split], in_=src[:, :split])
-            nc.vector.tensor_copy(out=dst[:, split:], in_=src[:, split:])
+            cuts = [0, split]
+            for lo, hi in zip(cuts, cuts[1:]):
+                nc.scalar.copy(out=dst[:, lo:hi], in_=src[:, lo:hi])
+            if split < P:
+                nc.vector.tensor_copy(out=dst[:, split:], in_=src[:, split:])
+
+        def cast_last(e, s):
+            g = placed([P, PACK * H], BF16, "wa_bf%d_%d" % (e, s), bf_at(e * PASSES + s))
+            grouped[e, s] = g
+            dst = g[:].rearrange("p (t m j) -> p m j t", t=PACK, j=PACK)
+            src = wa_raw[e, s][:].rearrange("p j (m t) -> p m j t", t=PACK)
+            nc.vector.tensor_copy(out=dst[:, :, :, 0:2], in_=src[:, :, :, 0:2])
+            nc.scalar.copy(out=dst[:, :LAST_V, :, 2:4], in_=src[:, :LAST_V, :, 2:4])
+            if LAST_V < P:
+                nc.vector.tensor_copy(out=dst[:, LAST_V:, :, 2:4], in_=src[:, LAST_V:, :, 2:4])
 
         def quant_wa(e, s):
             codes[e, s] = ring.tile([P, H], U32, name="wa_codes", align_bytes=64)
             scales[e, s] = ring.tile([P, H], U8, name="wa_scales", align_bytes=64)
             nc.vector.quantize_mx(out=codes[e, s][:].bitcast(FP8X4), scales=scales[e, s][:], in_=grouped[e, s][:])
 
-        def mm_wa(e, s):
+        def mm_wa(e, s, ts):
             for u in range(2):
                 if s == 0:
                     h_ps[e, u] = psum.tile([P, PACK, HALF], F32, name="h_ps%d" % u)
                 cols = slice(u * HALF, (u + 1) * HALF)
-                for t in range(PACK):
+                for t in ts:
                     m = slice(t * P, (t + 1) * P)
                     nc.tensor.matmul_mx(
                         out=h_ps[e, u][:, t, :],
@@ -148,28 +185,36 @@ def tile_moe_elr_relu_kernel(
                         start=(s == 0 and t == 0), stop=(s == PASSES - 1 and t == PACK - 1),
                     )
 
-        def mm_w(e, s):
-            for u in range(2):
-                if s == 0:
-                    y_ps[e, u] = psum.tile([P, HALF], F32, name="y_ps%d" % u)
-                cols = slice(u * HALF, (u + 1) * HALF)
-                slots = slice(e * C + u * HALF, e * C + (u + 1) * HALF)
-                plane = xsg[:, slots] if s == 0 else xs0[:, s - 1, slots]
-                nc.tensor.matmul_mx(
-                    out=y_ps[e, u][:],
-                    lhsT=ww[:, e * PASSES + s, :].bitcast(FP4X4), lhsT_scale=ws[:, e * PASSES + s, :],
-                    rhs=xg[e, s][:, cols].bitcast(FP8X4), rhs_scale=plane,
-                    start=(s == 0), stop=False,
-                )
+        wb_bf, wb_codes, wb_scales, h_bf, h_codes, h_scales = {}, {}, {}, {}, {}, {}
+        y_tiles = [ypsum.tile([P, w], F32, name="y_ps%d" % k) for k, w in enumerate((C, C, C, HALF))]
+        y_first = [0, C, 2 * C, 3 * C, 3 * C + HALF]
 
-        wb_bf, wb_codes, wb_scales, h_bf = {}, {}, {}, {}
+        def y_place(slot):
+            k = max(j for j in range(5) if y_first[j] <= slot)
+            return k, slot - y_first[k]
+
+        def mm_w(e):
+            for u in range(2):
+                slot = e * C + u * HALF
+                k, col = y_place(slot)
+                for s in range(PASSES):
+                    slots = slice(slot, slot + HALF)
+                    plane = xsg[:, slots] if s == 0 else xs0[:, s - 1, slots]
+                    nc.tensor.matmul_mx(
+                        out=y_tiles[k][:, col : col + HALF],
+                        lhsT=ww[e][:, s, :].bitcast(FP4X4), lhsT_scale=ws[:, e * PASSES + s, :],
+                        rhs=xg[e, s][:, u * HALF : (u + 1) * HALF].bitcast(FP8X4), rhs_scale=plane,
+                        start=(s == 0 and col == 0 and W_FIRST[e]), stop=(s == PASSES - 1 and (u == 1 or e == E - 1) and not W_FIRST[e]),
+                    )
 
         def cast_wb(e):
             wb_bf[e] = ring.tile([P, PACK * N], BF16, name="wb_bf", align_bytes=64)
-            nc.vector.tensor_copy(
-                out=wb_bf[e][:].rearrange("p (c i j) -> p c j i", i=4, j=PACK),
-                in_=wb_raw[e][:].rearrange("p j (c i) -> p c j i", i=4),
-            )
+            dst = wb_bf[e][:].rearrange("p (c i j) -> p c j i", i=4, j=PACK)
+            src = wb_raw[e][:].rearrange("p j (c i) -> p c j i", i=4)
+            if WB_ENG[e] == "S":
+                nc.scalar.copy(out=dst, in_=src)
+            else:
+                nc.vector.tensor_copy(out=dst, in_=src)
 
         def quant_wb(e):
             wb_codes[e] = ring.tile([P, N], U32, name="wb_codes", align_bytes=64)
@@ -177,80 +222,137 @@ def tile_moe_elr_relu_kernel(
             nc.vector.quantize_mx(out=wb_codes[e][:].bitcast(FP8X4), scales=wb_scales[e][:], in_=wb_bf[e][:])
 
         def relu_h(e, u, on_vector):
-            if e < E - 1:
-                h_bf[e, u] = placed([P, HALF, PACK], BF16, "h_bf%d_%d" % (e, u), raw_at(PASSES * (e + 1)) + u * HALF * PACK * 2)
-            else:
-                h_bf[e, u] = kept([P, HALF, PACK], BF16, "h_bf%d_%d" % (e, u))
+            if u == 0:
+                if e < E - 1:
+                    h_bf[e] = placed([P, C, PACK], BF16, "h_bf%d" % e, raw_at(PASSES * (e + 1) + RELU_LAG[e]))
+                else:
+                    h_bf[e] = kept([P, C, PACK], BF16, "h_bf%d" % e)
+                h_codes[e] = kept([P, C], U32, "h_codes%d" % e)
+                h_scales[e] = kept([P, C], U8, "h_scales%d" % e)
+            dst = h_bf[e][:, u * HALF : (u + 1) * HALF, :]
             src = h_ps[e, u][:].rearrange("p t n -> p n t")
             if on_vector:
-                nc.vector.tensor_scalar_max(out=h_bf[e, u][:], in0=src, scalar1=0.0)
+                nc.vector.tensor_scalar_max(out=dst, in0=src, scalar1=0.0)
             else:
-                nc.scalar.activation(out=h_bf[e, u][:], in_=src, func=RELU)
+                nc.scalar.activation(out=dst, in_=src, func=RELU)
 
-        def second(e, u, on_vector):
-            hc = ring.tile([P, HALF], U32, name="h_codes", align_bytes=64)
-            hs = ring.tile([P, HALF], U8, name="h_scales", align_bytes=64)
-            nc.vector.quantize_mx(out=hc[:].bitcast(FP8X4), scales=hs[:], in_=h_bf[e, u][:].rearrange("p n t -> p (n t)"))
-            nc.tensor.matmul_mx(
-                out=y_ps[e, u][:],
-                lhsT=wb_codes[e][:].bitcast(FP8X4), lhsT_scale=wb_scales[e][:],
-                rhs=hc[:].bitcast(FP8X4), rhs_scale=hs[:],
-                start=False, stop=True,
+        def quant_h(e, lo, hi):
+            nc.vector.quantize_mx(
+                out=h_codes[e][:, lo:hi].bitcast(FP8X4), scales=h_scales[e][:, lo:hi],
+                in_=h_bf[e][:, lo:hi, :].rearrange("p n t -> p (n t)"),
             )
-            dst = y_sb[:, e * C + u * HALF : e * C + (u + 1) * HALF]
+
+        def mm_wb(e, lo, hi):
+            k, col = y_place(e * C + lo)
+            width = hi - lo
+            nc.tensor.matmul_mx(
+                out=y_tiles[k][:, col : col + width],
+                lhsT=wb_codes[e][:].bitcast(FP8X4), lhsT_scale=wb_scales[e][:],
+                rhs=h_codes[e][:, lo:hi].bitcast(FP8X4), rhs_scale=h_scales[e][:, lo:hi],
+                start=not W_FIRST[e], stop=W_FIRST[e],
+            )
+
+        def copy_y(k, on_vector):
+            dst = y_sb[:, y_first[k] : y_first[k] + y_tiles[k].shape[1]]
             if on_vector:
-                nc.vector.tensor_copy(out=dst, in_=y_ps[e, u][:])
+                nc.vector.tensor_copy(out=dst, in_=y_tiles[k][:])
             else:
-                nc.scalar.copy(out=dst, in_=y_ps[e, u][:])
+                nc.scalar.copy(out=dst, in_=y_tiles[k][:])
 
         steps = [(e, s) for e in range(E) for s in range(PASSES)]
         last = len(steps) - 1
         gather(0, 0)
-        cast_wa(0, 0, SPLIT)
-        gather_scales()
-        load_ws(2)
+        cast_wa(0, 0, SPLITS[0])
+        gather_scales(0)
         load_wa(1, 1)
-        load_ws(3)
+        load_ws(0)
+        load_ws(1)
         load_wa(1, 2)
-        load_wb(1)
+        load_ws(2)
+        load_ws(3)
         for i, (e, s) in enumerate(steps):
             if i > 0:
                 gather(e, s)
             if i < last:
-                cast_wa(steps[i + 1][0], steps[i + 1][1], SPLIT if i + 1 < last else 44)
-            quant_wa(e, s)
-            mm_wa(e, s)
-            if s == 0 and e > 0:
-                second(e - 1, 0, False)
-                second(e - 1, 1, False)
-            if s == PASSES - 1:
-                for s2 in range(PASSES):
-                    mm_w(e, s2)
+                if i + 1 < last:
+                    cast_wa(steps[i + 1][0], steps[i + 1][1], SPLITS[i + 1])
+                else:
+                    cast_last(steps[last][0], steps[last][1])
+            if i < last:
+                quant_wa(e, s)
+                mm_wa(e, s, range(PACK))
+            else:
+                codes[e, s] = ring.tile([P, H], U32, name="wa_codes", align_bytes=64)
+                scales[e, s] = ring.tile([P, H], U8, name="wa_scales", align_bytes=64)
+                for th in range(2):
+                    cols = slice(th * H // 2, (th + 1) * H // 2)
+                    nc.vector.quantize_mx(
+                        out=codes[e, s][:, cols].bitcast(FP8X4), scales=scales[e, s][:, cols],
+                        in_=grouped[e, s][:, th * 2 * H : (th + 1) * 2 * H],
+                    )
+                    mm_wa(e, s, (2 * th, 2 * th + 1))
+            if i < E - 1:
+                gather_scales(i + 1)
+            if i == E - 2:
+                shift_scales()
+            for e2 in range(E - 1):
+                if i == PASSES * e2 + PASSES + RELU_LAG[e2]:
+                    quant_h(e2, 0, C)
+                if i == PASSES * e2 + PASSES - 1 + RELU_LAG[e2]:
+                    relu_h(e2, 0, False)
+                    relu_h(e2, 1, False)
+            if i == last:
                 relu_h(e, 0, False)
-                cast_wb(e)
-                relu_h(e, 1, e == E - 1)
-                quant_wb(e)
-            if i + 6 <= last:
-                load_wa(steps[i + 6][0], steps[i + 6][1])
-                if steps[i + 6][1] == PASSES - 1:
-                    load_wb(steps[i + 6][0])
-            if i + 6 == last:
+                relu_h(e, 1, LAST_RELU_V)
+            if i + RAW_SLOTS <= last:
+                load_wa(steps[i + RAW_SLOTS][0], steps[i + RAW_SLOTS][1])
+            if i == POS_AT:
                 nc.sync.dma_start(pos1_sb[:], pos1)
                 nc.sync.dma_start(pos2_sb[:], pos2)
-            if i == 8:
-                for r in range(2):
-                    gate_sb.append(placed([P, T], F32, "gate%d" % r, bf_at(8) + r * T * 4))
-                    nc.sync.dma_start(out=gate_sb[r][:], in_=gate[r])
-        second(E - 1, 0, False)
-        second(E - 1, 1, True)
+            if i == 8 + 1:
+                for item in LATE:
+                    if item[0] == "b":
+                        load_wb(int(item[1]))
+                    else:
+                        load_ww(int(item[1]), int(item[-1]) + 1, bf_at(7) + C * 4 + int(item[1]) * 768)
+            if i == 8 + 2:
+                gate_sb = placed([P, 2, T], F32, "gate_sb", bf_at(8 + 2))
+                nc.sync.dma_start(out=gate_sb[:], in_=gate.rearrange("r p t -> p r t"))
 
-        for b in range(2):
-            tok = slice(b * (T // 2), (b + 1) * (T // 2))
-            lst = slice(b * (T // 32), (b + 1) * (T // 32))
-            part1 = ring.tile([P, T // 2], F32, name="part1")
-            part2 = ring.tile([P, T // 2], F32, name="part2")
+        y_tiles.append(psum.tile([P, HALF], F32, name="h_ps0"))
+        for item in TAIL:
+            e = int(item[1])
+            if item[0] == "c":
+                cast_wb(e)
+            elif item[0] == "q":
+                quant_wb(e)
+            elif item[0] == "w":
+                mm_w(e)
+            elif item[0] == "h":
+                quant_h(E - 1, e * HALF, (e + 1) * HALF)
+            elif e < E - 1:
+                mm_wb(e, 0, C)
+            else:
+                mm_wb(e, 0, HALF)
+                mm_wb(e, HALF, C)
+        for j in YC_ORDER:
+            copy_y(j, YC_ENG[j] == "V")
+
+        parts = {}
+
+        def fetch(b, r):
+            lst = (pos1_sb, pos2_sb)[r][:, b * (T // 32) : (b + 1) * (T // 32)]
+            parts[b, r] = ring.tile([P, T // 2], F32, name="part")
+            nc.vector.tensor_tensor(parts[b, r][:], y_sb[:].indirect(lst), gate_sb[:, r, b * (T // 2) : (b + 1) * (T // 2)], ALU.mult)
+
+        def combine(b):
             res = ring.tile([P, T // 2], F32, name="res")
-            nc.vector.tensor_tensor(part1[:], y_sb[:].indirect(pos1_sb[:, lst]), gate_sb[0][:, tok], ALU.mult)
-            nc.vector.tensor_tensor(part2[:], y_sb[:].indirect(pos2_sb[:, lst]), gate_sb[1][:, tok], ALU.mult)
-            nc.vector.tensor_tensor(res[:], part1[:], part2[:], ALU.add)
-            nc.sync.dma_start(out=out[:, tok], in_=res[:])
+            nc.vector.tensor_tensor(res[:], parts[b, 0][:], parts[b, 1][:], ALU.add)
+            nc.sync.dma_start(out=out[:, b * (T // 2) : (b + 1) * (T // 2)], in_=res[:])
+
+        fetch(0, 0)
+        fetch(0, 1)
+        fetch(1, 0)
+        combine(0)
+        fetch(1, 1)
+        combine(1)

@@ -20,18 +20,18 @@ P = 128
 PACK = 4
 PASSES = K // (P * PACK)
 HALF = 128
-SPLITS = [128,128,128,100,48,84,104,64,64,52,44]
-HEAD = ["wa00","offs","xw0","xs3","xs1","xs2","xw1","wa01","xw2","xs0","wa02","wa10"]
-ACT_HEAD = "w"
+SPLITS = [120,128,128,128,40,104,116,40,76,64,52]
+HEAD = ["wa00","offs","xw0","xw1","xs3","wa01","xs2","xs1","xw2","wa02","wa10"]
+ACT_HEAD = "0w"
 WB_ENG = "SVVS"
-YC_ENG = "SVVVS"
-YC_ORDER = [0,4,1,2,3]
+YC_ENG = "SSVSV"
+YC_ORDER = [0,2,1,4,3]
 LATE = ["w01","b0","b3","b1","w3","b2","w2"]
-W_FIRST = [True,True,True,True]
-TAIL = ["c0","w2","h0","c1","q1","c3","q3","q0","w3","h1","w1","c2","m3","m1","w0","q2","m0","m2"]
-POS_AT = 0
+W_FIRST = [False,True,True,True]
+TAIL = ["h0","c0","w3","c1","q0","c3","q3","q1","c2","h1","q2","m0","w0","w1","m1","w2","m3","m2"]
+POS_AT = 3
 RELU_LAG = [1,0,1]
-LAST_V = 96
+LAST_V = 128
 LAST_RELU_V = False
 FREE_G = 8
 G_LAG = 6
@@ -154,7 +154,9 @@ def tile_moe_elr_relu_kernel(
             for lo, hi in zip(cuts, cuts[1:]):
                 nc.scalar.copy(out=dst[:, lo:hi], in_=src[:, lo:hi])
             if split < P:
-                nc.vector.tensor_copy(out=dst[:, split:], in_=src[:, split:])
+                dst = g[:].rearrange("p (h t m j) -> p h m j t", h=2, t=2, j=PACK)
+                src = wa_raw[e, s][:].rearrange("p j (m h t) -> p h m j t", h=2, t=2)
+                nc.vector.tensor_copy(out=dst[:, :, split:], in_=src[:, :, split:])
 
         def cast_last(e, s):
             g = placed([P, PACK * H], BF16, "wa_bf%d_%d" % (e, s), bf_at(e * PASSES + s))

@@ -21,7 +21,7 @@ PACK = 4
 PASSES = K // (P * PACK)
 HALF = 128
 SPLITS = [120,128,128,128,40,104,116,40,76,64,52]
-HEAD = ["wa00","offs","xw0","xw1","xs3","wa01","xs2","xs1","xw2","wa02","wa10"]
+HEAD = ["ws","wa00","offs","xw0","xw1","xs3","wa01","xs2","xs1","xw2","wa02","wa10"]
 ACT_HEAD = "0w"
 WB_ENG = "SVVS"
 YC_ENG = "SSVSV"
@@ -29,7 +29,8 @@ YC_ORDER = [0,2,1,4,3]
 LATE = ["w01","b0","b3","b1","w3","b2","w2"]
 W_FIRST = [False,True,True,True]
 TAIL = ["h0","c0","w3","c1","q0","c3","q3","q1","c2","h1","q2","m0","w0","w1","m1","w2","m3","m2"]
-POS_AT = 3
+POS_AT = 0
+LG = 6
 RELU_LAG = [1,0,1]
 LAST_V = 128
 LAST_RELU_V = False
@@ -90,10 +91,10 @@ def tile_moe_elr_relu_kernel(
                 load_xs(int(item), nc.scalar)
         nc.vector.memset(ws[:].rearrange("p a n -> p (a n)").bitcast(I32), 0)
         nc.vector.memset(xs0[:].rearrange("p a n -> p (a n)").bitcast(I32), 0)
-        ws_rows = w_scales.bitcast(I32).rearrange("e s (q r) w -> r q (e s) w", r=4)
+        ws_rows = keep.tile([16, E * PASSES, N], U8, name="ws_rows")
 
-        def load_ws(r):
-            nc.sync.dma_start(out=ws[r:P:32, :, :].bitcast(I32), in_=ws_rows[r])
+        def spread_ws(q):
+            nc.sync.dma_start(out=ws[32 * q : 32 * q + 4, :, :].bitcast(I32), in_=ws_rows[4 * q : 4 * q + 4, :, :].bitcast(I32))
 
         def load_wa(e, s, pieces=((0, H),)):
             if (e, s) not in wa_raw:
@@ -103,7 +104,7 @@ def tile_moe_elr_relu_kernel(
                 nc.sync.dma_start(out=wa_raw[e, s][:, :, lo:hi], in_=rows[:, :, lo:hi])
 
         def load_wb(e):
-            wb_raw[e] = placed([P, PACK, N], F32, "wb_raw%d" % e, bf_at(8) + [x for x in LATE if x[0] == "b"].index("b%d" % e) * PACK * N * 4)
+            wb_raw[e] = placed([P, PACK, N], F32, "wb_raw%d" % e, bf_at(LG) + [x for x in LATE if x[0] == "b"].index("b%d" % e) * PACK * N * 4)
             nc.sync.dma_start(out=wb_raw[e][:], in_=wb[e].rearrange("(p j) c -> p j c", j=PACK))
 
         ww = {}
@@ -118,7 +119,9 @@ def tile_moe_elr_relu_kernel(
             nc.sync.dma_start(out=xw[s][:], in_=x_words[s].rearrange("p t d -> p (t d)").bitcast(I32))
 
         for item in HEAD:
-            if item == "offs":
+            if item == "ws":
+                nc.sync.dma_start(out=ws_rows[:].bitcast(I32), in_=w_scales.bitcast(I32).rearrange("e s b w -> b (e s) w"))
+            elif item == "offs":
                 nc.sync.dma_start(offs_sb[:], offs)
             elif item[:2] == "xw":
                 load_xw(int(item[2]))
@@ -267,11 +270,7 @@ def tile_moe_elr_relu_kernel(
         cast_wa(0, 0, SPLITS[0])
         gather_scales(0)
         load_wa(1, 1)
-        load_ws(0)
-        load_ws(1)
         load_wa(1, 2)
-        load_ws(2)
-        load_ws(3)
         for i, (e, s) in enumerate(steps):
             if i > 0:
                 gather(e, s)
@@ -308,18 +307,21 @@ def tile_moe_elr_relu_kernel(
                 relu_h(e, 1, LAST_RELU_V)
             if i + RAW_SLOTS <= last:
                 load_wa(steps[i + RAW_SLOTS][0], steps[i + RAW_SLOTS][1])
-            if i == POS_AT:
-                nc.sync.dma_start(pos1_sb[:], pos1)
-                nc.sync.dma_start(pos2_sb[:], pos2)
-            if i == 8 + 1:
+            if POS_AT <= i < POS_AT + 4:
+                spread_ws(i - POS_AT)
+            if i == LG + 1:
                 for item in LATE:
                     if item[0] == "b":
                         load_wb(int(item[1]))
                     else:
-                        load_ww(int(item[1]), int(item[-1]) + 1, bf_at(7) + C * 4 + int(item[1]) * 768)
-            if i == 8 + 2:
-                gate_sb = placed([P, 2, T], F32, "gate_sb", bf_at(8 + 2))
-                nc.sync.dma_start(out=gate_sb[:], in_=gate.rearrange("r p t -> p r t"))
+                        load_ww(int(item[1]), int(item[-1]) + 1, bf_at(LG - 1) + C * 4 + int(item[1]) * 768)
+            if i == LG + 2:
+                gate_sb = placed([P, 2, T], F32, "gate_sb", bf_at(LG + 2))
+                nc.sync.dma_start(pos1_sb[:], pos1)
+                nc.sync.dma_start(pos2_sb[:], pos2)
+                for b in range(2):
+                    tok = slice(b * (T // 2), (b + 1) * (T // 2))
+                    nc.sync.dma_start(out=gate_sb[:, :, tok], in_=gate.rearrange("r p t -> p r t")[:, :, tok])
 
         y_tiles.append(psum.tile([P, HALF], F32, name="h_ps0"))
         for item in TAIL:

@@ -27,10 +27,11 @@ WB_ENG = "SVVS"
 YC_ENG = "SSVSV"
 YC_ORDER = [0,2,1,4,3]
 LATE = ["w01","b0","b3","b1","w3","b2","w2"]
-W_FIRST = [False,True,True,True]
-TAIL = ["h0","c0","w3","c1","q0","c3","q3","q1","c2","h1","q2","m0","w0","w1","m1","w2","m3","m2"]
+W_FIRST = [True,True,True,True]
+TAIL = ["h0","c0","w0","w1","w3","c1","q0","c3","q3","q1","c2","h1","q2","m0","m1","w2","m3","m2"]
 POS_AT = 0
 LG = 6
+BUSY_AT = (8, 9)
 RELU_LAG = [1,0,1]
 LAST_V = 128
 LAST_RELU_V = False
@@ -191,6 +192,18 @@ def tile_moe_elr_relu_kernel(
                     )
 
         wb_bf, wb_codes, wb_scales, h_bf, h_codes, h_scales = {}, {}, {}, {}, {}, {}
+        spare = ypsum.tile([P, 2, C], F32, name="y_ps2")
+
+        def keep_busy(e, s):
+            for t in range(PACK):
+                m = slice(t * P, (t + 1) * P)
+                nc.tensor.matmul_mx(
+                    out=spare[:, t % 2, :],
+                    lhsT=codes[e, s][:, m].bitcast(FP8X4), lhsT_scale=scales[e, s][:, m],
+                    rhs=xg[e, s][:].bitcast(FP8X4), rhs_scale=xsg[4 * s :, e * C : (e + 1) * C],
+                    start=True, stop=True,
+                )
+
         y_tiles = [ypsum.tile([P, w], F32, name="y_ps%d" % k) for k, w in enumerate((C, C, C, HALF))]
         y_first = [0, C, 2 * C, 3 * C, 3 * C + HALF]
 
@@ -282,6 +295,8 @@ def tile_moe_elr_relu_kernel(
             if i < last:
                 quant_wa(e, s)
                 mm_wa(e, s, range(PACK))
+                if i in BUSY_AT:
+                    keep_busy(e, s)
             else:
                 codes[e, s] = ring.tile([P, H], U32, name="wa_codes", align_bytes=64)
                 scales[e, s] = ring.tile([P, H], U8, name="wa_scales", align_bytes=64)

@@ -19,28 +19,15 @@ ALU = mybir.AluOpType
 P = 128
 PACK = 4
 PASSES = K // (P * PACK)
-HALF = 128
-SPLITS = [120,128,128,128,40,104,116,40,76,64,52]
-HEAD = ["ws","wa00","offs","xw0","xw1","xs3","wa01","xs2","xs1","xw2","wa02","wa10"]
-ACT_HEAD = "0w"
-WB_ENG = "SVVS"
-YC_ENG = "SSVSV"
-YC_ORDER = [0,2,1,4,3]
-LATE = ["w01","b0","b3","b1","w3","b2","w2"]
-W_FIRST = [True,True,True,True]
-TAIL = ["h0","c0","w0","w1","w3","c1","q0","c3","q3","q1","c2","h1","q2","m0","m1","w2","m3","m2"]
-POS_AT = 0
-LG = 6
-BUSY_AT = (8, 9)
-RELU_LAG = [1,0,1]
-LAST_V = 128
-LAST_RELU_V = False
-FREE_G = 8
-G_LAG = 6
-WW_AT = 1
-RAW_SLOTS = 6
-RAW_BYTES = PACK * H * 4
-BF_BYTES = PACK * H * 2
+HALF = C // 2
+QUADS = 4
+LIST = 16
+SHIFT_ROWS = 112
+BF_BUFS = 6
+PAIR = 2 * C
+WINDOW = 704
+SCALAR_ALONE = 4
+EARLY = 1
 
 
 def tile_moe_elr_relu_kernel(
@@ -49,323 +36,243 @@ def tile_moe_elr_relu_kernel(
     nc = tc.nc
     with ExitStack() as ctx:
         keep = ctx.enter_context(tc.tile_pool(name="keep", bufs=1))
-        ring = ctx.enter_context(tc.tile_pool(name="ring", bufs=4))
-        arena = ctx.enter_context(tc.tile_pool(name="arena", bufs=1))
-        psum = ctx.enter_context(tc.psum_pool(name="psum", bufs=2))
+        ring = ctx.enter_context(tc.tile_pool(name="ring", bufs=BF_BUFS))
+        hpsum = ctx.enter_context(tc.psum_pool(name="hpsum", bufs=2))
         ypsum = ctx.enter_context(tc.psum_pool(name="ypsum", bufs=1))
 
         def kept(shape, dtype, name):
             return keep.tile(shape, dtype, name=name, align_bytes=64)
 
-        def placed(shape, dtype, name, offset):
-            return arena.tile(shape, dtype, name=name, align_bytes=64, offset=offset)
-
-        def raw_at(i):
-            return (i % RAW_SLOTS) * RAW_BYTES
-
-        def bf_at(i):
-            return RAW_SLOTS * RAW_BYTES + i * BF_BYTES
-
-        offs_sb = keep.tile([P, E * C // 16], U16, name="offs_sb")
-        pos1_sb = keep.tile([P, T // 16], U16, name="pos1_sb")
-        pos2_sb = keep.tile([P, T // 16], U16, name="pos2_sb")
-        xw = [kept([P, T], I32, "xw%d" % s) for s in range(PASSES)]
-        xs = kept([P, T], U8, "xs")
+        offs_sb = keep.tile([P, E * C // LIST], U16, name="offs_sb")
+        pos_sb = [keep.tile([P, T // LIST], U16, name="pos%d_sb" % r) for r in range(2)]
+        xw = [kept([P, WINDOW], I32, "xw%d" % s) for s in range(PASSES)]
+        xs = kept([P, WINDOW], U8, "xs")
         xsg = kept([P, E * C], U8, "xsg")
-        xs0 = kept([P, PASSES - 1, E * C], U8, "xs0")
+        xs_low = [kept([P, E * C], U8, "xs_low%d" % s) for s in range(1, PASSES)]
+        ws_rows = keep.tile([4 * QUADS, E * PASSES, N], U8, name="ws_rows")
         ws = kept([P, E * PASSES, N], U8, "ws")
-        wa_raw = {}
-        wb_raw = {}
         y_sb = kept([P, E * C], F32, "y_sb")
+        gate_sb = [kept([P, 2, T // 2], F32, "gate%d" % b) for b in range(2)]
 
-        warm = kept([P, 8], F32, "warm")
         nc.vector.memset(xs[:].bitcast(I32), 0)
-        nc.vector.memset(warm[:, 0:1], 0.0)
-
-        def load_xs(q, engine):
-            engine.dma_start(out=xs[32 * q : 32 * q + 4 * PASSES, :].bitcast(I32), in_=x_scales.bitcast(I32)[:, 4 * q : 4 * q + 4, :])
-
-        for item in ACT_HEAD:
-            if item == "w":
-                nc.scalar.activation(out=warm[:, 1:2], in_=warm[:, 0:1], func=RELU)
-            else:
-                load_xs(int(item), nc.scalar)
+        for s in range(PASSES):
+            nc.vector.memset(xw[s][:, T:], 0)
         nc.vector.memset(ws[:].rearrange("p a n -> p (a n)").bitcast(I32), 0)
-        nc.vector.memset(xs0[:].rearrange("p a n -> p (a n)").bitcast(I32), 0)
-        ws_rows = keep.tile([16, E * PASSES, N], U8, name="ws_rows")
+        for plane in xs_low:
+            nc.vector.memset(plane[:].bitcast(I32), 0)
+
+        nc.sync.dma_start(offs_sb[:], offs)
+        for s in range(PASSES):
+            nc.sync.dma_start(out=xw[s][:, :T], in_=x_words[s].rearrange("p t d -> p (t d)").bitcast(I32))
+        for q in range(QUADS):
+            nc.scalar.dma_start(
+                out=xs[32 * q : 32 * q + 4 * PASSES, :T].bitcast(I32), in_=x_scales.bitcast(I32)[:, 4 * q : 4 * q + 4, :]
+            )
+
+        xg = {}
+        pairs = range(E * C // PAIR)
+        lists = [offs_sb[:, b * (PAIR // LIST) : (b + 1) * (PAIR // LIST)] for b in pairs]
+        for b in pairs:
+            nc.vector.tensor_copy(xsg[:, b * PAIR : (b + 1) * PAIR], xs[:].indirect(lists[b]))
+
+        def gather_words(b, s, name):
+            words = kept([P, PAIR], U32, name)
+            nc.vector.tensor_copy(words[:], xw[s][:].bitcast(U32).indirect(lists[b]))
+            for i in range(2):
+                xg[2 * b + i, s] = words[:, i * C : (i + 1) * C]
+
+        for s in range(PASSES):
+            gather_words(0, s, "xg%d" % s)
+
+        def load_ws_rows():
+            nc.sync.dma_start(out=ws_rows[:].bitcast(I32), in_=w_scales.bitcast(I32).rearrange("e s b w -> b (e s) w"))
 
         def spread_ws(q):
             nc.sync.dma_start(out=ws[32 * q : 32 * q + 4, :, :].bitcast(I32), in_=ws_rows[4 * q : 4 * q + 4, :, :].bitcast(I32))
 
-        def load_wa(e, s, pieces=((0, H),)):
-            if (e, s) not in wa_raw:
-                wa_raw[e, s] = placed([P, PACK, H], F32, "wa_raw%d_%d" % (e, s), raw_at(e * PASSES + s))
-            rows = wa[e, 512 * s : 512 * (s + 1), :].rearrange("(p j) c -> p j c", j=PACK)
-            for lo, hi in pieces:
-                nc.sync.dma_start(out=wa_raw[e, s][:, :, lo:hi], in_=rows[:, :, lo:hi])
+        def lower_xs(s):
+            nc.sync.dma_start(
+                out=xs_low[s - 1][0:SHIFT_ROWS, :].bitcast(I32), in_=xsg[4 * s : 4 * s + SHIFT_ROWS, :].bitcast(I32)
+            )
+
+        small_moves = [load_ws_rows]
+        small_moves.extend([lambda q=q: spread_ws(q) for q in range(QUADS)])
+        small_moves.extend([lambda s=s: lower_xs(s) for s in range(1, PASSES)])
+
+        wa_raw, wb_raw, ww = {}, {}, {}
 
         def load_wb(e):
-            wb_raw[e] = placed([P, PACK, N], F32, "wb_raw%d" % e, bf_at(LG) + [x for x in LATE if x[0] == "b"].index("b%d" % e) * PACK * N * 4)
+            wb_raw[e] = kept([P, PACK, N], F32, "wb_raw%d" % e)
             nc.sync.dma_start(out=wb_raw[e][:], in_=wb[e].rearrange("(p j) c -> p j c", j=PACK))
 
-        ww = {}
+        def load_ww(e):
+            ww[e] = kept([P, PASSES, 2 * N], U8, "ww%d" % e)
+            nc.sync.dma_start(out=ww[e][:].bitcast(I32), in_=w_words[e].bitcast(I32).rearrange("s p w -> p s w"))
 
-        def load_ww(lo, hi, offset):
-            words = placed([P, (hi - lo) * PASSES, 2 * N], U8, "ww%d" % lo, offset)
-            for e in range(lo, hi):
-                ww[e] = words[:, (e - lo) * PASSES : (e - lo + 1) * PASSES, :]
-            nc.sync.dma_start(out=words[:].bitcast(I32), in_=w_words[lo:hi].bitcast(I32).rearrange("e s p w -> p (e s) w"))
+        for e in range(E):
+            for s in range(PASSES):
+                wa_raw[e, s] = kept([P, PACK, H], F32, "wa_raw%d_%d" % (e, s))
+                rows = wa[e, 512 * s : 512 * (s + 1), :].rearrange("(p j) c -> p j c", j=PACK)
+                nc.sync.dma_start(out=wa_raw[e, s][:], in_=rows)
+                at = e * PASSES + s - PASSES
+                if 0 <= at < len(small_moves):
+                    small_moves[at]()
+            if e < EARLY:
+                load_wb(e)
+                load_ww(e)
+        last = E - 1
+        middle = range(EARLY, last)
+        load_wb(last)
+        for e in middle:
+            load_wb(e)
+        for e in range(EARLY, E):
+            load_ww(e)
+        nc.sync.dma_start(pos_sb[0][:], pos1)
+        nc.sync.dma_start(pos_sb[1][:], pos2)
+        for b in range(2):
+            tok = slice(b * (T // 2), (b + 1) * (T // 2))
+            nc.sync.dma_start(out=gate_sb[b][:], in_=gate.rearrange("r p t -> p r t")[:, :, tok])
 
-        def load_xw(s):
-            nc.sync.dma_start(out=xw[s][:], in_=x_words[s].rearrange("p t d -> p (t d)").bitcast(I32))
+        h_ps = {}
+        wb_codes, wb_scales, h_codes, h_scales = {}, {}, {}, {}
 
-        for item in HEAD:
-            if item == "ws":
-                nc.sync.dma_start(out=ws_rows[:].bitcast(I32), in_=w_scales.bitcast(I32).rearrange("e s b w -> b (e s) w"))
-            elif item == "offs":
-                nc.sync.dma_start(offs_sb[:], offs)
-            elif item[:2] == "xw":
-                load_xw(int(item[2]))
-            elif item[:2] == "xs":
-                load_xs(int(item[2]), nc.sync)
+        def cast_wa(e, s):
+            grouped = ring.tile([P, PACK * H], BF16, name="wa_bf", align_bytes=64)
+            dst = grouped[:].rearrange("p (g t m j) -> p g m j t", g=2, t=2, j=PACK)
+            src = wa_raw[e, s][:].rearrange("p j (m g t) -> p g m j t", g=2, t=2)
+            if e * PASSES + s < SCALAR_ALONE:
+                nc.scalar.copy(out=dst, in_=src)
             else:
-                load_wa(int(item[2]), int(item[3]))
+                nc.vector.tensor_copy(out=dst[:, 0], in_=src[:, 0])
+                nc.scalar.copy(out=dst[:, 1], in_=src[:, 1])
+            return grouped
 
-        xg, grouped, codes, scales, h_ps = {}, {}, {}, {}, {}
-
-        def gather(e, s):
-            lst = offs_sb[:, e * (C // 16) : (e + 1) * (C // 16)]
-            if e * PASSES + s < FREE_G:
-                xg[e, s] = kept([P, C], U32, "xg%d_%d" % (e, s))
-            else:
-                xg[e, s] = placed([P, C], U32, "xg%d_%d" % (e, s), bf_at(e * PASSES + s - G_LAG))
-            nc.vector.tensor_copy(xg[e, s][:], xw[s][:].bitcast(U32).indirect(lst))
-
-        def gather_scales(e):
-            lst = offs_sb[:, e * (C // 16) : (e + 1) * (C // 16)]
-            nc.vector.tensor_copy(xsg[:, e * C : (e + 1) * C], xs[:].indirect(lst))
-
-        def shift_scales():
-            for s in range(1, PASSES):
-                nc.sync.dma_start(out=xs0[0:112, s - 1, :].bitcast(I32), in_=xsg[4 * s : 4 * s + 112, :].bitcast(I32))
-
-        def cast_wa(e, s, split):
-            g = placed([P, PACK * H], BF16, "wa_bf%d_%d" % (e, s), bf_at(e * PASSES + s))
-            grouped[e, s] = g
-            dst = g[:].rearrange("p (t m j) -> p m j t", t=PACK, j=PACK)
-            src = wa_raw[e, s][:].rearrange("p j (m t) -> p m j t", t=PACK)
-            cuts = [0, split]
-            for lo, hi in zip(cuts, cuts[1:]):
-                nc.scalar.copy(out=dst[:, lo:hi], in_=src[:, lo:hi])
-            if split < P:
-                dst = g[:].rearrange("p (h t m j) -> p h m j t", h=2, t=2, j=PACK)
-                src = wa_raw[e, s][:].rearrange("p j (m h t) -> p h m j t", h=2, t=2)
-                nc.vector.tensor_copy(out=dst[:, :, split:], in_=src[:, :, split:])
-
-        def cast_last(e, s):
-            g = placed([P, PACK * H], BF16, "wa_bf%d_%d" % (e, s), bf_at(e * PASSES + s))
-            grouped[e, s] = g
-            dst = g[:].rearrange("p (t m j) -> p m j t", t=PACK, j=PACK)
-            src = wa_raw[e, s][:].rearrange("p j (m t) -> p m j t", t=PACK)
-            nc.vector.tensor_copy(out=dst[:, :, :, 0:2], in_=src[:, :, :, 0:2])
-            nc.scalar.copy(out=dst[:, :LAST_V, :, 2:4], in_=src[:, :LAST_V, :, 2:4])
-            if LAST_V < P:
-                nc.vector.tensor_copy(out=dst[:, LAST_V:, :, 2:4], in_=src[:, LAST_V:, :, 2:4])
-
-        def quant_wa(e, s):
-            codes[e, s] = ring.tile([P, H], U32, name="wa_codes", align_bytes=64)
-            scales[e, s] = ring.tile([P, H], U8, name="wa_scales", align_bytes=64)
-            nc.vector.quantize_mx(out=codes[e, s][:].bitcast(FP8X4), scales=scales[e, s][:], in_=grouped[e, s][:])
-
-        def mm_wa(e, s, ts):
+        def mm_wa(e, s, codes, scales, ts):
             for u in range(2):
                 if s == 0:
-                    h_ps[e, u] = psum.tile([P, PACK, HALF], F32, name="h_ps%d" % u)
-                cols = slice(u * HALF, (u + 1) * HALF)
+                    h_ps[e, u] = hpsum.tile([P, PACK, HALF], F32, name="h_ps%d" % u)
                 for t in ts:
                     m = slice(t * P, (t + 1) * P)
                     nc.tensor.matmul_mx(
                         out=h_ps[e, u][:, t, :],
-                        lhsT=codes[e, s][:, m].bitcast(FP8X4), lhsT_scale=scales[e, s][:, m],
-                        rhs=xg[e, s][:, cols].bitcast(FP8X4), rhs_scale=xsg[4 * s :, e * C + u * HALF : e * C + (u + 1) * HALF],
+                        lhsT=codes[:, m].bitcast(FP8X4), lhsT_scale=scales[:, m],
+                        rhs=xg[e, s][:, u * HALF : (u + 1) * HALF].bitcast(FP8X4),
+                        rhs_scale=xsg[4 * s :, e * C + u * HALF : e * C + (u + 1) * HALF],
                         start=(s == 0 and t == 0), stop=(s == PASSES - 1 and t == PACK - 1),
                     )
 
-        wb_bf, wb_codes, wb_scales, h_bf, h_codes, h_scales = {}, {}, {}, {}, {}, {}
-        spare = ypsum.tile([P, 2, C], F32, name="y_ps2")
-
-        def keep_busy(e, s):
-            for t in range(PACK):
-                m = slice(t * P, (t + 1) * P)
-                nc.tensor.matmul_mx(
-                    out=spare[:, t % 2, :],
-                    lhsT=codes[e, s][:, m].bitcast(FP8X4), lhsT_scale=scales[e, s][:, m],
-                    rhs=xg[e, s][:].bitcast(FP8X4), rhs_scale=xsg[4 * s :, e * C : (e + 1) * C],
-                    start=True, stop=True,
+        def step_wa(e, s):
+            grouped = cast_wa(e, s)
+            codes = ring.tile([P, H], U32, name="wa_codes", align_bytes=64)
+            scales = ring.tile([P, H], U8, name="wa_scales", align_bytes=64)
+            pieces = 2 if (e, s) == (E - 1, PASSES - 1) else 1
+            width = H // pieces
+            for g in range(pieces):
+                cols = slice(g * width, (g + 1) * width)
+                nc.vector.quantize_mx(
+                    out=codes[:, cols].bitcast(FP8X4), scales=scales[:, cols],
+                    in_=grouped[:, g * PACK * width : (g + 1) * PACK * width],
                 )
+                mm_wa(e, s, codes, scales, range(g * PACK // pieces, (g + 1) * PACK // pieces))
 
-        y_tiles = [ypsum.tile([P, w], F32, name="y_ps%d" % k) for k, w in enumerate((C, C, C, HALF))]
-        y_first = [0, C, 2 * C, 3 * C, 3 * C + HALF]
+        wb_bf = {}
 
-        def y_place(slot):
-            k = max(j for j in range(5) if y_first[j] <= slot)
-            return k, slot - y_first[k]
-
-        def mm_w(e):
-            for u in range(2):
-                slot = e * C + u * HALF
-                k, col = y_place(slot)
-                for s in range(PASSES):
-                    slots = slice(slot, slot + HALF)
-                    plane = xsg[:, slots] if s == 0 else xs0[:, s - 1, slots]
-                    nc.tensor.matmul_mx(
-                        out=y_tiles[k][:, col : col + HALF],
-                        lhsT=ww[e][:, s, :].bitcast(FP4X4), lhsT_scale=ws[:, e * PASSES + s, :],
-                        rhs=xg[e, s][:, u * HALF : (u + 1) * HALF].bitcast(FP8X4), rhs_scale=plane,
-                        start=(s == 0 and col == 0 and W_FIRST[e]), stop=(s == PASSES - 1 and (u == 1 or e == E - 1) and not W_FIRST[e]),
-                    )
-
-        def cast_wb(e):
-            wb_bf[e] = ring.tile([P, PACK * N], BF16, name="wb_bf", align_bytes=64)
+        def cast_wb(e, on_vector):
+            wb_bf[e] = kept([P, PACK * N], BF16, "wb_bf%d" % e)
             dst = wb_bf[e][:].rearrange("p (c i j) -> p c j i", i=4, j=PACK)
             src = wb_raw[e][:].rearrange("p j (c i) -> p c j i", i=4)
-            if WB_ENG[e] == "S":
-                nc.scalar.copy(out=dst, in_=src)
-            else:
+            if on_vector:
                 nc.vector.tensor_copy(out=dst, in_=src)
+            else:
+                nc.scalar.copy(out=dst, in_=src)
 
         def quant_wb(e):
-            wb_codes[e] = ring.tile([P, N], U32, name="wb_codes", align_bytes=64)
-            wb_scales[e] = ring.tile([P, N], U8, name="wb_scales", align_bytes=64)
+            wb_codes[e] = kept([P, N], U32, "wb_codes%d" % e)
+            wb_scales[e] = kept([P, N], U8, "wb_scales%d" % e)
             nc.vector.quantize_mx(out=wb_codes[e][:].bitcast(FP8X4), scales=wb_scales[e][:], in_=wb_bf[e][:])
 
-        def relu_h(e, u, on_vector):
-            if u == 0:
-                if e < E - 1:
-                    h_bf[e] = placed([P, C, PACK], BF16, "h_bf%d" % e, raw_at(PASSES * (e + 1) + RELU_LAG[e]))
+        def hidden(e):
+            h_bf = kept([P, C, PACK], BF16, "wa_raw%d_0" % min(e + 1, E - 1) if e < E - 1 else "h_bf")
+            h_codes[e] = kept([P, C], U32, "h_codes%d" % e)
+            h_scales[e] = kept([P, C], U8, "h_scales%d" % e)
+            for u in range(2):
+                dst = h_bf[:, u * HALF : (u + 1) * HALF, :]
+                src = h_ps[e, u][:].rearrange("p t n -> p n t")
+                if e == E - 1 and u == 1:
+                    nc.vector.tensor_scalar_max(out=dst, in0=src, scalar1=0.0)
                 else:
-                    h_bf[e] = kept([P, C, PACK], BF16, "h_bf%d" % e)
-                h_codes[e] = kept([P, C], U32, "h_codes%d" % e)
-                h_scales[e] = kept([P, C], U8, "h_scales%d" % e)
-            dst = h_bf[e][:, u * HALF : (u + 1) * HALF, :]
-            src = h_ps[e, u][:].rearrange("p t n -> p n t")
-            if on_vector:
-                nc.vector.tensor_scalar_max(out=dst, in0=src, scalar1=0.0)
-            else:
-                nc.scalar.activation(out=dst, in_=src, func=RELU)
+                    nc.scalar.activation(out=dst, in_=src, func=RELU)
+            pieces = 2 if e == E - 1 else 1
+            width = C // pieces
+            for g in range(pieces):
+                cols = slice(g * width, (g + 1) * width)
+                nc.vector.quantize_mx(
+                    out=h_codes[e][:, cols].bitcast(FP8X4), scales=h_scales[e][:, cols],
+                    in_=h_bf[:, cols, :].rearrange("p n t -> p (n t)"),
+                )
 
-        def quant_h(e, lo, hi):
-            nc.vector.quantize_mx(
-                out=h_codes[e][:, lo:hi].bitcast(FP8X4), scales=h_scales[e][:, lo:hi],
-                in_=h_bf[e][:, lo:hi, :].rearrange("p n t -> p (n t)"),
-            )
-
-        def mm_wb(e, lo, hi):
-            k, col = y_place(e * C + lo)
-            width = hi - lo
+        def mm_wb(e, target, cols, start, stop):
             nc.tensor.matmul_mx(
-                out=y_tiles[k][:, col : col + width],
+                out=target,
                 lhsT=wb_codes[e][:].bitcast(FP8X4), lhsT_scale=wb_scales[e][:],
-                rhs=h_codes[e][:, lo:hi].bitcast(FP8X4), rhs_scale=h_scales[e][:, lo:hi],
-                start=not W_FIRST[e], stop=W_FIRST[e],
+                rhs=h_codes[e][:, cols].bitcast(FP8X4), rhs_scale=h_scales[e][:, cols],
+                start=start, stop=stop,
             )
 
-        def copy_y(k, on_vector):
-            dst = y_sb[:, y_first[k] : y_first[k] + y_tiles[k].shape[1]]
-            if on_vector:
-                nc.vector.tensor_copy(out=dst, in_=y_tiles[k][:])
-            else:
-                nc.scalar.copy(out=dst, in_=y_tiles[k][:])
+        def mm_w(e, u, target, start, stop):
+            slots = slice(e * C + u * HALF, e * C + (u + 1) * HALF)
+            for s in range(PASSES):
+                plane = xsg if s == 0 else xs_low[s - 1]
+                nc.tensor.matmul_mx(
+                    out=target,
+                    lhsT=ww[e][:, s, :].bitcast(FP4X4), lhsT_scale=ws[:, e * PASSES + s, :],
+                    rhs=xg[e, s][:, u * HALF : (u + 1) * HALF].bitcast(FP8X4), rhs_scale=plane[:, slots],
+                    start=(start and s == 0), stop=(stop and s == PASSES - 1),
+                )
 
-        steps = [(e, s) for e in range(E) for s in range(PASSES)]
-        last = len(steps) - 1
-        gather(0, 0)
-        cast_wa(0, 0, SPLITS[0])
-        gather_scales(0)
-        load_wa(1, 1)
-        load_wa(1, 2)
-        for i, (e, s) in enumerate(steps):
-            if i > 0:
-                gather(e, s)
-            if i < last:
-                if i + 1 < last:
-                    cast_wa(steps[i + 1][0], steps[i + 1][1], SPLITS[i + 1])
-                else:
-                    cast_last(steps[last][0], steps[last][1])
-            if i < last:
-                quant_wa(e, s)
-                mm_wa(e, s, range(PACK))
-                if i in BUSY_AT:
-                    keep_busy(e, s)
-            else:
-                codes[e, s] = ring.tile([P, H], U32, name="wa_codes", align_bytes=64)
-                scales[e, s] = ring.tile([P, H], U8, name="wa_scales", align_bytes=64)
-                for th in range(2):
-                    cols = slice(th * H // 2, (th + 1) * H // 2)
-                    nc.vector.quantize_mx(
-                        out=codes[e, s][:, cols].bitcast(FP8X4), scales=scales[e, s][:, cols],
-                        in_=grouped[e, s][:, th * 2 * H : (th + 1) * 2 * H],
-                    )
-                    mm_wa(e, s, (2 * th, 2 * th + 1))
-            if i < E - 1:
-                gather_scales(i + 1)
-            if i == E - 2:
-                shift_scales()
-            for e2 in range(E - 1):
-                if i == PASSES * e2 + PASSES + RELU_LAG[e2]:
-                    quant_h(e2, 0, C)
-                if i == PASSES * e2 + PASSES - 1 + RELU_LAG[e2]:
-                    relu_h(e2, 0, False)
-                    relu_h(e2, 1, False)
-            if i == last:
-                relu_h(e, 0, False)
-                relu_h(e, 1, LAST_RELU_V)
-            if i + RAW_SLOTS <= last:
-                load_wa(steps[i + RAW_SLOTS][0], steps[i + RAW_SLOTS][1])
-            if POS_AT <= i < POS_AT + 4:
-                spread_ws(i - POS_AT)
-            if i == LG + 1:
-                for item in LATE:
-                    if item[0] == "b":
-                        load_wb(int(item[1]))
-                    else:
-                        load_ww(int(item[1]), int(item[-1]) + 1, bf_at(LG - 1) + C * 4 + int(item[1]) * 768)
-            if i == LG + 2:
-                gate_sb = placed([P, 2, T], F32, "gate_sb", bf_at(LG + 2))
-                nc.sync.dma_start(pos1_sb[:], pos1)
-                nc.sync.dma_start(pos2_sb[:], pos2)
-                for b in range(2):
-                    tok = slice(b * (T // 2), (b + 1) * (T // 2))
-                    nc.sync.dma_start(out=gate_sb[:, :, tok], in_=gate.rearrange("r p t -> p r t")[:, :, tok])
+        def finish(e):
+            y_ps = ypsum.tile([P, C], F32, name="y_ps%d" % e)
+            for u in range(2):
+                mm_w(e, u, y_ps[:, u * HALF : (u + 1) * HALF], u == 0, False)
+            mm_wb(e, y_ps[:], slice(0, C), False, True)
+            nc.scalar.copy(out=y_sb[:, e * C : (e + 1) * C], in_=y_ps[:])
 
-        y_tiles.append(psum.tile([P, HALF], F32, name="h_ps0"))
-        for item in TAIL:
-            e = int(item[1])
-            if item[0] == "c":
-                cast_wb(e)
-            elif item[0] == "q":
-                quant_wb(e)
-            elif item[0] == "w":
-                mm_w(e)
-            elif item[0] == "h":
-                quant_h(E - 1, e * HALF, (e + 1) * HALF)
-            elif e < E - 1:
-                mm_wb(e, 0, C)
-            else:
-                mm_wb(e, 0, HALF)
-                mm_wb(e, HALF, C)
-        for j in YC_ORDER:
-            copy_y(j, YC_ENG[j] == "V")
+        for e in range(E):
+            for s in range(PASSES):
+                step_wa(e, s)
+                if e == 0:
+                    gather_words(1, s, "wa_raw%d_%d" % (e, s))
+                if e > 0 and s == 0:
+                    hidden(e - 1)
+                    if e - 1 < EARLY:
+                        cast_wb(e - 1, False)
+                        quant_wb(e - 1)
+                        finish(e - 1)
+
+        hidden(last)
+        cast_wb(last, False)
+        quant_wb(last)
+        for e in middle:
+            cast_wb(e, e == last - 1)
+            quant_wb(e)
+        y_last = [ypsum.tile([P, HALF], F32, name="y_ps%d" % last), hpsum.tile([P, HALF], F32, name="h_ps0")]
+        for u in range(2):
+            mm_w(last, u, y_last[u][:], True, False)
+            mm_wb(last, y_last[u][:], slice(u * HALF, (u + 1) * HALF), False, True)
+        for e in middle:
+            finish(e)
+        nc.scalar.copy(out=y_sb[:, last * C : last * C + HALF], in_=y_last[0][:])
+        nc.vector.tensor_copy(out=y_sb[:, last * C + HALF :], in_=y_last[1][:])
 
         parts = {}
 
         def fetch(b, r):
-            lst = (pos1_sb, pos2_sb)[r][:, b * (T // 32) : (b + 1) * (T // 32)]
-            parts[b, r] = ring.tile([P, T // 2], F32, name="part")
-            nc.vector.tensor_tensor(parts[b, r][:], y_sb[:].indirect(lst), gate_sb[:, r, b * (T // 2) : (b + 1) * (T // 2)], ALU.mult)
+            lst = pos_sb[r][:, b * (T // 2 // LIST) : (b + 1) * (T // 2 // LIST)]
+            parts[b, r] = kept([P, T // 2], F32, "part%d_%d" % (b, r))
+            nc.vector.tensor_tensor(parts[b, r][:], y_sb[:].indirect(lst), gate_sb[b][:, r, :], ALU.mult)
 
         def combine(b):
-            res = ring.tile([P, T // 2], F32, name="res")
+            res = kept([P, T // 2], F32, "res%d" % b)
             nc.vector.tensor_tensor(res[:], parts[b, 0][:], parts[b, 1][:], ALU.add)
             nc.sync.dma_start(out=out[:, b * (T // 2) : (b + 1) * (T // 2)], in_=res[:])
 

@@ -148,7 +148,7 @@ def tile_moe_elr_relu_kernel(
             return grouped
 
         def mm_wa(e, s, codes, scales, ts):
-            for u in range(2):
+            for u in (1, 0):
                 if s == 0:
                     h_ps[e, u] = hpsum.tile([P, PACK, HALF], F32, name="h_ps%d" % u)
                 for t in ts:
@@ -198,13 +198,13 @@ def tile_moe_elr_relu_kernel(
             for u in range(2):
                 dst = h_bf[:, u * HALF : (u + 1) * HALF, :]
                 src = h_ps[e, u][:].rearrange("p t n -> p n t")
-                if e == E - 1 and u == 1:
+                if u == 1:
                     nc.vector.tensor_scalar_max(out=dst, in0=src, scalar1=0.0)
                 else:
                     nc.scalar.activation(out=dst, in_=src, func=RELU)
             pieces = 2 if e == E - 1 else 1
             width = C // pieces
-            for g in range(pieces):
+            for g in reversed(range(pieces)):
                 cols = slice(g * width, (g + 1) * width)
                 nc.vector.quantize_mx(
                     out=h_codes[e][:, cols].bitcast(FP8X4), scales=h_scales[e][:, cols],
@@ -245,7 +245,7 @@ def tile_moe_elr_relu_kernel(
                 if e > 0 and s == 0:
                     hidden(e - 1)
                     if e - 1 < EARLY:
-                        cast_wb(e - 1, False)
+                        cast_wb(e - 1, True)
                         quant_wb(e - 1)
                         finish(e - 1)
 
@@ -255,14 +255,17 @@ def tile_moe_elr_relu_kernel(
         for e in middle:
             cast_wb(e, e == last - 1)
             quant_wb(e)
-        y_last = [ypsum.tile([P, HALF], F32, name="y_ps%d" % last), hpsum.tile([P, HALF], F32, name="h_ps0")]
+        late = range(EARLY, E)
+        y_end = [ypsum.tile([P, len(late), HALF], F32, name="y_end%d" % u) for u in range(2)]
         for u in range(2):
-            mm_w(last, u, y_last[u][:], True, False)
-            mm_wb(last, y_last[u][:], slice(u * HALF, (u + 1) * HALF), False, True)
-        for e in middle:
-            finish(e)
-        nc.scalar.copy(out=y_sb[:, last * C : last * C + HALF], in_=y_last[0][:])
-        nc.vector.tensor_copy(out=y_sb[:, last * C + HALF :], in_=y_last[1][:])
+            for i, e in enumerate(late):
+                mm_w(e, u, y_end[u][:, i, :], i == 0, False)
+        for i, e in enumerate(late):
+            for u in (1, 0):
+                mm_wb(e, y_end[u][:, i, :], slice(u * HALF, (u + 1) * HALF), False, e == last)
+        y_late = y_sb[:, EARLY * C :].rearrange("p (e u n) -> p u e n", u=2, n=HALF)
+        nc.vector.tensor_copy(out=y_late[:, 1], in_=y_end[1][:])
+        nc.scalar.copy(out=y_late[:, 0], in_=y_end[0][:])
 
         parts = {}
 

@@ -27,7 +27,7 @@ BF_BUFS = 6
 PAIR = 2 * C
 WINDOW = 704
 SCALAR_ALONE = 4
-EARLY = 1
+TAIL = 128
 
 
 def tile_moe_elr_relu_kernel(
@@ -49,10 +49,10 @@ def tile_moe_elr_relu_kernel(
         xs = kept([P, WINDOW], U8, "xs")
         xsg = kept([P, E * C], U8, "xsg")
         xs_low = [kept([P, E * C], U8, "xs_low%d" % s) for s in range(1, PASSES)]
-        ws_rows = keep.tile([4 * QUADS, E * PASSES, N], U8, name="ws_rows")
         ws = kept([P, E * PASSES, N], U8, "ws")
         y_sb = kept([P, E * C], F32, "y_sb")
-        gate_sb = [kept([P, 2, T // 2], F32, "gate%d" % b) for b in range(2)]
+        spans = [slice(0, T - TAIL), slice(T - TAIL, T)]
+        gate_sb = [kept([P, 2, tok.stop - tok.start], F32, "gate%d" % b) for b, tok in enumerate(spans)]
 
         nc.vector.memset(xs[:].bitcast(I32), 0)
         for s in range(PASSES):
@@ -84,19 +84,16 @@ def tile_moe_elr_relu_kernel(
         for s in range(PASSES):
             gather_words(0, s, "xg%d" % s)
 
-        def load_ws_rows():
-            nc.sync.dma_start(out=ws_rows[:].bitcast(I32), in_=w_scales.bitcast(I32).rearrange("e s b w -> b (e s) w"))
-
-        def spread_ws(q):
-            nc.sync.dma_start(out=ws[32 * q : 32 * q + 4, :, :].bitcast(I32), in_=ws_rows[4 * q : 4 * q + 4, :, :].bitcast(I32))
+        def load_ws(q):
+            rows = w_scales.bitcast(I32).rearrange("e s b w -> b (e s) w")
+            nc.sync.dma_start(out=ws[32 * q : 32 * q + 4, :, :].bitcast(I32), in_=rows[4 * q : 4 * q + 4, :, :])
 
         def lower_xs(s):
             nc.sync.dma_start(
                 out=xs_low[s - 1][0:SHIFT_ROWS, :].bitcast(I32), in_=xsg[4 * s : 4 * s + SHIFT_ROWS, :].bitcast(I32)
             )
 
-        small_moves = [load_ws_rows]
-        small_moves.extend([lambda q=q: spread_ws(q) for q in range(QUADS)])
+        small_moves = [lambda q=q: load_ws(q) for q in range(QUADS)]
         small_moves.extend([lambda s=s: lower_xs(s) for s in range(1, PASSES)])
 
         wa_raw, wb_raw, ww = {}, {}, {}
@@ -105,9 +102,11 @@ def tile_moe_elr_relu_kernel(
             wb_raw[e] = kept([P, PACK, N], F32, "wb_raw%d" % e)
             nc.sync.dma_start(out=wb_raw[e][:], in_=wb[e].rearrange("(p j) c -> p j c", j=PACK))
 
-        def load_ww(e):
-            ww[e] = kept([P, PASSES, 2 * N], U8, "ww%d" % e)
-            nc.sync.dma_start(out=ww[e][:].bitcast(I32), in_=w_words[e].bitcast(I32).rearrange("s p w -> p s w"))
+        def load_ww(lo, hi):
+            words = kept([P, (hi - lo) * PASSES, 2 * N], U8, "ww%d" % lo)
+            nc.sync.dma_start(out=words[:].bitcast(I32), in_=w_words[lo:hi].bitcast(I32).rearrange("e s p w -> p (e s) w"))
+            for e in range(lo, hi):
+                ww[e] = words[:, (e - lo) * PASSES : (e - lo + 1) * PASSES, :]
 
         for e in range(E):
             for s in range(PASSES):
@@ -117,20 +116,15 @@ def tile_moe_elr_relu_kernel(
                 at = e * PASSES + s - PASSES
                 if 0 <= at < len(small_moves):
                     small_moves[at]()
-            if e < EARLY:
-                load_wb(e)
-                load_ww(e)
         last = E - 1
-        middle = range(EARLY, last)
-        load_wb(last)
-        for e in middle:
+        wb_order = [0, 1, last, last - 1]
+        load_ww(0, last)
+        for e in wb_order:
             load_wb(e)
-        for e in range(EARLY, E):
-            load_ww(e)
+        load_ww(last, E)
         nc.sync.dma_start(pos_sb[0][:], pos1)
         nc.sync.dma_start(pos_sb[1][:], pos2)
-        for b in range(2):
-            tok = slice(b * (T // 2), (b + 1) * (T // 2))
+        for b, tok in enumerate(spans):
             nc.sync.dma_start(out=gate_sb[b][:], in_=gate.rearrange("r p t -> p r t")[:, :, tok])
 
         h_ps = {}
@@ -230,12 +224,13 @@ def tile_moe_elr_relu_kernel(
                     start=(start and s == 0), stop=(stop and s == PASSES - 1),
                 )
 
-        def finish(e):
+        def finish(e, on_vector):
             y_ps = ypsum.tile([P, C], F32, name="y_ps%d" % e)
             for u in range(2):
                 mm_w(e, u, y_ps[:, u * HALF : (u + 1) * HALF], u == 0, False)
             mm_wb(e, y_ps[:], slice(0, C), False, True)
-            nc.scalar.copy(out=y_sb[:, e * C : (e + 1) * C], in_=y_ps[:])
+            copy = nc.vector.tensor_copy if on_vector else nc.scalar.copy
+            copy(out=y_sb[:, e * C : (e + 1) * C], in_=y_ps[:])
 
         for e in range(E):
             for s in range(PASSES):
@@ -244,40 +239,32 @@ def tile_moe_elr_relu_kernel(
                     gather_words(1, s, "wa_raw%d_%d" % (e, s))
                 if e > 0 and s == 0:
                     hidden(e - 1)
-                    if e - 1 < EARLY:
-                        cast_wb(e - 1, True)
-                        quant_wb(e - 1)
-                        finish(e - 1)
 
         hidden(last)
-        cast_wb(last, False)
-        quant_wb(last)
-        for e in middle:
-            cast_wb(e, e == last - 1)
+        for e in wb_order:
+            cast_wb(e, e == wb_order[-1])
             quant_wb(e)
-        late = range(EARLY, E)
-        y_end = [ypsum.tile([P, len(late), HALF], F32, name="y_end%d" % u) for u in range(2)]
-        for u in range(2):
-            for i, e in enumerate(late):
-                mm_w(e, u, y_end[u][:, i, :], i == 0, False)
-        for i, e in enumerate(late):
-            for u in (1, 0):
-                mm_wb(e, y_end[u][:, i, :], slice(u * HALF, (u + 1) * HALF), False, e == last)
-        y_late = y_sb[:, EARLY * C :].rearrange("p (e u n) -> p u e n", u=2, n=HALF)
-        nc.vector.tensor_copy(out=y_late[:, 1], in_=y_end[1][:])
-        nc.scalar.copy(out=y_late[:, 0], in_=y_end[0][:])
+        y_last = [ypsum.tile([P, HALF], F32, name="y_ps%d" % last), hpsum.tile([P, HALF], F32, name="h_ps0")]
+        for u in (1, 0):
+            mm_w(last, u, y_last[u][:], True, False)
+        for u in (1, 0):
+            mm_wb(last, y_last[u][:], slice(u * HALF, (u + 1) * HALF), False, True)
+        nc.vector.tensor_copy(out=y_sb[:, last * C + HALF :], in_=y_last[1][:])
+        nc.scalar.copy(out=y_sb[:, last * C : last * C + HALF], in_=y_last[0][:])
+        for e in range(last):
+            finish(e, e == wb_order[-1])
 
         parts = {}
 
         def fetch(b, r):
-            lst = pos_sb[r][:, b * (T // 2 // LIST) : (b + 1) * (T // 2 // LIST)]
-            parts[b, r] = kept([P, T // 2], F32, "part%d_%d" % (b, r))
+            lst = pos_sb[r][:, spans[b].start // LIST : spans[b].stop // LIST]
+            parts[b, r] = kept([P, spans[b].stop - spans[b].start], F32, "part%d_%d" % (b, r))
             nc.vector.tensor_tensor(parts[b, r][:], y_sb[:].indirect(lst), gate_sb[b][:, r, :], ALU.mult)
 
         def combine(b):
-            res = kept([P, T // 2], F32, "res%d" % b)
+            res = kept([P, spans[b].stop - spans[b].start], F32, "res%d" % b)
             nc.vector.tensor_tensor(res[:], parts[b, 0][:], parts[b, 1][:], ALU.add)
-            nc.sync.dma_start(out=out[:, b * (T // 2) : (b + 1) * (T // 2)], in_=res[:])
+            nc.sync.dma_start(out=out[:, spans[b]], in_=res[:])
 
         fetch(0, 0)
         fetch(0, 1)

@@ -93,9 +93,6 @@ def tile_moe_elr_relu_kernel(
                 out=xs_low[s - 1][0:SHIFT_ROWS, :].bitcast(I32), in_=xsg[4 * s : 4 * s + SHIFT_ROWS, :].bitcast(I32)
             )
 
-        small_moves = [lambda q=q: load_ws(q) for q in range(QUADS)]
-        small_moves.extend([lambda s=s: lower_xs(s) for s in range(1, PASSES)])
-
         wa_raw, wb_raw, ww = {}, {}, {}
 
         def load_wb(e):
@@ -113,13 +110,15 @@ def tile_moe_elr_relu_kernel(
                 wa_raw[e, s] = kept([P, PACK, H], F32, "wa_raw%d_%d" % (e, s))
                 rows = wa[e, 512 * s : 512 * (s + 1), :].rearrange("(p j) c -> p j c", j=PACK)
                 nc.sync.dma_start(out=wa_raw[e, s][:], in_=rows)
-                at = e * PASSES + s - PASSES
-                if 0 <= at < len(small_moves):
-                    small_moves[at]()
         last = E - 1
         wb_order = [0, 1, last, last - 1]
+        load_wb(wb_order[0])
+        for s in range(1, PASSES):
+            lower_xs(s)
+        for q in range(QUADS):
+            load_ws(q)
         load_ww(0, last)
-        for e in wb_order:
+        for e in wb_order[1:]:
             load_wb(e)
         load_ww(last, E)
         nc.sync.dma_start(pos_sb[0][:], pos1)

@@ -18,15 +18,19 @@ ALU = mybir.AluOpType
 
 P = 128
 PACK = 4
-PASSES = K // (P * PACK)
+PASS_ROWS = P * PACK
+PASSES = K // PASS_ROWS
+LAST = E - 1
 HALF = C // 2
-QUADS = 4
-LIST = 16
-SHIFT_ROWS = 112
-BF_BUFS = 6
+QUAD = 32
+QUAD_ROWS = 4
+LIST_ROWS = 16
 PAIR = 2 * C
-WINDOW = 704
+WINDOW = T + 192
+MOVED_ROWS = 112
+RING = 6
 SCALAR_ALONE = 4
+VECTOR_WB = 2
 TAIL = 128
 
 
@@ -36,234 +40,229 @@ def tile_moe_elr_relu_kernel(
     nc = tc.nc
     with ExitStack() as ctx:
         keep = ctx.enter_context(tc.tile_pool(name="keep", bufs=1))
-        ring = ctx.enter_context(tc.tile_pool(name="ring", bufs=BF_BUFS))
+        ring = ctx.enter_context(tc.tile_pool(name="ring", bufs=RING))
         hpsum = ctx.enter_context(tc.psum_pool(name="hpsum", bufs=2))
         ypsum = ctx.enter_context(tc.psum_pool(name="ypsum", bufs=1))
 
         def kept(shape, dtype, name):
             return keep.tile(shape, dtype, name=name, align_bytes=64)
 
-        offs_sb = keep.tile([P, E * C // LIST], U16, name="offs_sb")
-        pos_sb = [keep.tile([P, T // LIST], U16, name="pos%d_sb" % r) for r in range(2)]
+        def half(u):
+            return slice(u * HALF, (u + 1) * HALF)
+
+        offs_sb = keep.tile([P, E * C // LIST_ROWS], U16, name="offs_sb")
+        pos_sb = [keep.tile([P, T // LIST_ROWS], U16, name="pos%d_sb" % r) for r in range(2)]
         xw = [kept([P, WINDOW], I32, "xw%d" % s) for s in range(PASSES)]
         xs = kept([P, WINDOW], U8, "xs")
         xsg = kept([P, E * C], U8, "xsg")
-        xs_low = [kept([P, E * C], U8, "xs_low%d" % s) for s in range(1, PASSES)]
+        xs_moved = {s: kept([P, E * C], U8, "xs_low%d" % s) for s in range(1, PASSES)}
         ws = kept([P, E * PASSES, N], U8, "ws")
         y_sb = kept([P, E * C], F32, "y_sb")
-        spans = [slice(0, T - TAIL), slice(T - TAIL, T)]
-        gate_sb = [kept([P, 2, tok.stop - tok.start], F32, "gate%d" % b) for b, tok in enumerate(spans)]
+        gate_sb = [kept([P, T], F32, "gate%d" % r) for r in range(2)]
 
         nc.vector.memset(xs[:].bitcast(I32), 0)
         for s in range(PASSES):
             nc.vector.memset(xw[s][:, T:], 0)
         nc.vector.memset(ws[:].rearrange("p a n -> p (a n)").bitcast(I32), 0)
-        for plane in xs_low:
-            nc.vector.memset(plane[:].bitcast(I32), 0)
+        for s in range(1, PASSES):
+            nc.vector.memset(xs_moved[s][:].bitcast(I32), 0)
 
         nc.sync.dma_start(offs_sb[:], offs)
         for s in range(PASSES):
             nc.sync.dma_start(out=xw[s][:, :T], in_=x_words[s].rearrange("p t d -> p (t d)").bitcast(I32))
-        for q in range(QUADS):
+        for q in range(P // QUAD):
             nc.scalar.dma_start(
-                out=xs[32 * q : 32 * q + 4 * PASSES, :T].bitcast(I32), in_=x_scales.bitcast(I32)[:, 4 * q : 4 * q + 4, :]
+                out=xs[QUAD * q : QUAD * q + QUAD_ROWS * PASSES, :T].bitcast(I32),
+                in_=x_scales.bitcast(I32)[:, QUAD_ROWS * q : QUAD_ROWS * (q + 1), :],
             )
 
         xg = {}
         pairs = range(E * C // PAIR)
-        lists = [offs_sb[:, b * (PAIR // LIST) : (b + 1) * (PAIR // LIST)] for b in pairs]
+        pair_list = [offs_sb[:, b * (PAIR // LIST_ROWS) : (b + 1) * (PAIR // LIST_ROWS)] for b in pairs]
         for b in pairs:
-            nc.vector.tensor_copy(xsg[:, b * PAIR : (b + 1) * PAIR], xs[:].indirect(lists[b]))
+            nc.vector.tensor_copy(xsg[:, b * PAIR : (b + 1) * PAIR], xs[:].indirect(pair_list[b]))
 
         def gather_words(b, s, name):
-            words = kept([P, PAIR], U32, name)
-            nc.vector.tensor_copy(words[:], xw[s][:].bitcast(U32).indirect(lists[b]))
+            gathered = kept([P, PAIR], U32, name)
+            nc.vector.tensor_copy(gathered[:], xw[s][:].bitcast(U32).indirect(pair_list[b]))
             for i in range(2):
-                xg[2 * b + i, s] = words[:, i * C : (i + 1) * C]
+                xg[2 * b + i, s] = gathered[:, i * C : (i + 1) * C]
 
         for s in range(PASSES):
             gather_words(0, s, "xg%d" % s)
 
-        def load_ws(q):
-            rows = w_scales.bitcast(I32).rearrange("e s b w -> b (e s) w")
-            nc.sync.dma_start(out=ws[32 * q : 32 * q + 4, :, :].bitcast(I32), in_=rows[4 * q : 4 * q + 4, :, :])
+        def load_ws(r):
+            rows = w_scales.bitcast(I32).rearrange("e s (q r) w -> r q (e s) w", r=QUAD_ROWS)
+            nc.sync.dma_start(out=ws[r:P:QUAD, :, :].bitcast(I32), in_=rows[r])
 
-        def lower_xs(s):
+        def move_plane(s):
+            first = QUAD_ROWS * s
             nc.sync.dma_start(
-                out=xs_low[s - 1][0:SHIFT_ROWS, :].bitcast(I32), in_=xsg[4 * s : 4 * s + SHIFT_ROWS, :].bitcast(I32)
+                out=xs_moved[s][0:MOVED_ROWS, :].bitcast(I32), in_=xsg[first : first + MOVED_ROWS, :].bitcast(I32)
             )
 
         wa_raw, wb_raw, ww = {}, {}, {}
+
+        def raw_name(e, s):
+            return "wa_raw%d_%d" % (e, s)
+
+        def load_wa(e, s):
+            wa_raw[e, s] = kept([P, PACK, H], F32, raw_name(e, s))
+            rows = wa[e, PASS_ROWS * s : PASS_ROWS * (s + 1), :].rearrange("(p j) c -> p j c", j=PACK)
+            nc.sync.dma_start(out=wa_raw[e, s][:], in_=rows)
 
         def load_wb(e):
             wb_raw[e] = kept([P, PACK, N], F32, "wb_raw%d" % e)
             nc.sync.dma_start(out=wb_raw[e][:], in_=wb[e].rearrange("(p j) c -> p j c", j=PACK))
 
         def load_ww(lo, hi):
-            words = kept([P, (hi - lo) * PASSES, 2 * N], U8, "ww%d" % lo)
-            nc.sync.dma_start(out=words[:].bitcast(I32), in_=w_words[lo:hi].bitcast(I32).rearrange("e s p w -> p (e s) w"))
+            fp4 = kept([P, (hi - lo) * PASSES, 2 * N], U8, "ww%d" % lo)
+            nc.sync.dma_start(out=fp4[:].bitcast(I32), in_=w_words[lo:hi].bitcast(I32).rearrange("e s p w -> p (e s) w"))
             for e in range(lo, hi):
-                ww[e] = words[:, (e - lo) * PASSES : (e - lo + 1) * PASSES, :]
+                ww[e] = fp4[:, (e - lo) * PASSES : (e - lo + 1) * PASSES, :]
 
-        for e in range(E):
-            for s in range(PASSES):
-                wa_raw[e, s] = kept([P, PACK, H], F32, "wa_raw%d_%d" % (e, s))
-                rows = wa[e, 512 * s : 512 * (s + 1), :].rearrange("(p j) c -> p j c", j=PACK)
-                nc.sync.dma_start(out=wa_raw[e, s][:], in_=rows)
-        last = E - 1
-        wb_order = [0, 1, last, last - 1]
-        load_wb(wb_order[0])
-        for s in range(1, PASSES):
-            lower_xs(s)
-        for q in range(QUADS):
-            load_ws(q)
-        load_ww(0, last)
-        for e in wb_order[1:]:
+        steps = [(e, s) for e in range(E) for s in range(PASSES)]
+        for e, s in steps[:-1]:
+            load_wa(e, s)
+        move_plane(1)
+        load_wa(*steps[-1])
+        load_wb(0)
+        move_plane(2)
+        for r in range(QUAD_ROWS):
+            load_ws(r)
+        load_ww(0, LAST)
+        for e in range(1, E):
             load_wb(e)
-        load_ww(last, E)
-        nc.sync.dma_start(pos_sb[0][:], pos1)
-        nc.sync.dma_start(pos_sb[1][:], pos2)
-        for b, tok in enumerate(spans):
-            nc.sync.dma_start(out=gate_sb[b][:], in_=gate.rearrange("r p t -> p r t")[:, :, tok])
+        load_ww(LAST, E)
+        for r, pos in enumerate((pos1, pos2)):
+            nc.sync.dma_start(pos_sb[r][:], pos)
+            nc.sync.dma_start(out=gate_sb[r][:], in_=gate[r])
 
         h_ps = {}
         wb_codes, wb_scales, h_codes, h_scales = {}, {}, {}, {}
 
-        def cast_wa(e, s):
-            grouped = ring.tile([P, PACK * H], BF16, name="wa_bf", align_bytes=64)
-            dst = grouped[:].rearrange("p (g t m j) -> p g m j t", g=2, t=2, j=PACK)
-            src = wa_raw[e, s][:].rearrange("p j (m g t) -> p g m j t", g=2, t=2)
+        def round_wa(e, s):
+            rounded = ring.tile([P, PACK * H], BF16, name="wa_bf", align_bytes=64)
+            dst = rounded[:].rearrange("p (g v m j) -> p g m j v", g=2, v=2, j=PACK)
+            src = wa_raw[e, s][:].rearrange("p j (m g v) -> p g m j v", g=2, v=2)
             if e * PASSES + s < SCALAR_ALONE:
                 nc.scalar.copy(out=dst, in_=src)
             else:
                 nc.vector.tensor_copy(out=dst[:, 0], in_=src[:, 0])
                 nc.scalar.copy(out=dst[:, 1], in_=src[:, 1])
-            return grouped
+            return rounded
 
-        def mm_wa(e, s, codes, scales, ts):
+        def mm_wa(e, s, codes, scales, outputs):
             for u in (1, 0):
                 if s == 0:
                     h_ps[e, u] = hpsum.tile([P, PACK, HALF], F32, name="h_ps%d" % u)
-                for t in ts:
+                for t in outputs:
                     m = slice(t * P, (t + 1) * P)
                     nc.tensor.matmul_mx(
                         out=h_ps[e, u][:, t, :],
                         lhsT=codes[:, m].bitcast(FP8X4), lhsT_scale=scales[:, m],
-                        rhs=xg[e, s][:, u * HALF : (u + 1) * HALF].bitcast(FP8X4),
-                        rhs_scale=xsg[4 * s :, e * C + u * HALF : e * C + (u + 1) * HALF],
+                        rhs=xg[e, s][:, half(u)].bitcast(FP8X4),
+                        rhs_scale=xsg[QUAD_ROWS * s :, e * C + u * HALF : e * C + (u + 1) * HALF],
                         start=(s == 0 and t == 0), stop=(s == PASSES - 1 and t == PACK - 1),
                     )
 
         def step_wa(e, s):
-            grouped = cast_wa(e, s)
+            rounded = round_wa(e, s)
             codes = ring.tile([P, H], U32, name="wa_codes", align_bytes=64)
             scales = ring.tile([P, H], U8, name="wa_scales", align_bytes=64)
-            pieces = 2 if (e, s) == (E - 1, PASSES - 1) else 1
+            pieces = 2 if (e, s) == steps[-1] else 1
             width = H // pieces
             for g in range(pieces):
                 cols = slice(g * width, (g + 1) * width)
                 nc.vector.quantize_mx(
                     out=codes[:, cols].bitcast(FP8X4), scales=scales[:, cols],
-                    in_=grouped[:, g * PACK * width : (g + 1) * PACK * width],
+                    in_=rounded[:, g * PACK * width : (g + 1) * PACK * width],
                 )
                 mm_wa(e, s, codes, scales, range(g * PACK // pieces, (g + 1) * PACK // pieces))
 
-        wb_bf = {}
-
-        def cast_wb(e, on_vector):
-            wb_bf[e] = kept([P, PACK * N], BF16, "wb_bf%d" % e)
-            dst = wb_bf[e][:].rearrange("p (c i j) -> p c j i", i=4, j=PACK)
-            src = wb_raw[e][:].rearrange("p j (c i) -> p c j i", i=4)
-            if on_vector:
+        def prepare_wb(e):
+            rounded = kept([P, PACK * N], BF16, "wb_bf%d" % e)
+            dst = rounded[:].rearrange("p (c n j) -> p c j n", n=4, j=PACK)
+            src = wb_raw[e][:].rearrange("p j (c n) -> p c j n", n=4)
+            if e >= E - VECTOR_WB:
                 nc.vector.tensor_copy(out=dst, in_=src)
             else:
                 nc.scalar.copy(out=dst, in_=src)
-
-        def quant_wb(e):
             wb_codes[e] = kept([P, N], U32, "wb_codes%d" % e)
             wb_scales[e] = kept([P, N], U8, "wb_scales%d" % e)
-            nc.vector.quantize_mx(out=wb_codes[e][:].bitcast(FP8X4), scales=wb_scales[e][:], in_=wb_bf[e][:])
+            nc.vector.quantize_mx(out=wb_codes[e][:].bitcast(FP8X4), scales=wb_scales[e][:], in_=rounded[:])
 
-        def hidden(e):
-            h_bf = kept([P, C, PACK], BF16, "wa_raw%d_0" % min(e + 1, E - 1) if e < E - 1 else "h_bf")
+        def hidden(e, name):
+            rounded = kept([P, C, PACK], BF16, name)
             h_codes[e] = kept([P, C], U32, "h_codes%d" % e)
             h_scales[e] = kept([P, C], U8, "h_scales%d" % e)
-            for u in range(2):
-                dst = h_bf[:, u * HALF : (u + 1) * HALF, :]
-                src = h_ps[e, u][:].rearrange("p t n -> p n t")
-                if u == 1:
-                    nc.vector.tensor_scalar_max(out=dst, in0=src, scalar1=0.0)
-                else:
-                    nc.scalar.activation(out=dst, in_=src, func=RELU)
-            pieces = 2 if e == E - 1 else 1
-            width = C // pieces
-            for g in reversed(range(pieces)):
-                cols = slice(g * width, (g + 1) * width)
+            by_slot = [h_ps[e, u][:].rearrange("p t n -> p n t") for u in range(2)]
+            nc.scalar.activation(out=rounded[:, half(0), :], in_=by_slot[0], func=RELU)
+            nc.vector.tensor_scalar_max(out=rounded[:, half(1), :], in0=by_slot[1], scalar1=0.0)
+            for cols in [half(1), half(0)] if e == LAST else [slice(0, C)]:
                 nc.vector.quantize_mx(
                     out=h_codes[e][:, cols].bitcast(FP8X4), scales=h_scales[e][:, cols],
-                    in_=h_bf[:, cols, :].rearrange("p n t -> p (n t)"),
+                    in_=rounded[:, cols, :].rearrange("p n t -> p (n t)"),
                 )
 
-        def mm_wb(e, target, cols, start, stop):
+        def mm_w(e, u, target, start):
+            slots = slice(e * C + u * HALF, e * C + (u + 1) * HALF)
+            for s in range(PASSES):
+                plane = xsg if s == 0 else xs_moved[s]
+                nc.tensor.matmul_mx(
+                    out=target,
+                    lhsT=ww[e][:, s, :].bitcast(FP4X4), lhsT_scale=ws[:, e * PASSES + s, :],
+                    rhs=xg[e, s][:, half(u)].bitcast(FP8X4), rhs_scale=plane[:, slots],
+                    start=(start and s == 0), stop=False,
+                )
+
+        def mm_wb(e, target, cols):
             nc.tensor.matmul_mx(
                 out=target,
                 lhsT=wb_codes[e][:].bitcast(FP8X4), lhsT_scale=wb_scales[e][:],
                 rhs=h_codes[e][:, cols].bitcast(FP8X4), rhs_scale=h_scales[e][:, cols],
-                start=start, stop=stop,
+                start=False, stop=True,
             )
 
-        def mm_w(e, u, target, start, stop):
-            slots = slice(e * C + u * HALF, e * C + (u + 1) * HALF)
-            for s in range(PASSES):
-                plane = xsg if s == 0 else xs_low[s - 1]
-                nc.tensor.matmul_mx(
-                    out=target,
-                    lhsT=ww[e][:, s, :].bitcast(FP4X4), lhsT_scale=ws[:, e * PASSES + s, :],
-                    rhs=xg[e, s][:, u * HALF : (u + 1) * HALF].bitcast(FP8X4), rhs_scale=plane[:, slots],
-                    start=(start and s == 0), stop=(stop and s == PASSES - 1),
-                )
+        for e, s in steps:
+            step_wa(e, s)
+            if e == 0:
+                gather_words(1, s, raw_name(e, s))
+            if e > 0 and s == 0:
+                hidden(e - 1, raw_name(e, s))
 
-        def finish(e, on_vector):
+        hidden(LAST, "h_bf")
+        for e in range(E):
+            prepare_wb(e)
+
+        y_last = [ypsum.tile([P, HALF], F32, name="y_ps%d" % LAST), hpsum.tile([P, HALF], F32, name="h_ps0")]
+        for u in (1, 0):
+            mm_w(LAST, u, y_last[u][:], True)
+        for u in (1, 0):
+            mm_wb(LAST, y_last[u][:], half(u))
+        nc.vector.tensor_copy(out=y_sb[:, LAST * C + HALF :], in_=y_last[1][:])
+        nc.scalar.copy(out=y_sb[:, LAST * C : LAST * C + HALF], in_=y_last[0][:])
+        for e in range(LAST):
             y_ps = ypsum.tile([P, C], F32, name="y_ps%d" % e)
             for u in range(2):
-                mm_w(e, u, y_ps[:, u * HALF : (u + 1) * HALF], u == 0, False)
-            mm_wb(e, y_ps[:], slice(0, C), False, True)
-            copy = nc.vector.tensor_copy if on_vector else nc.scalar.copy
-            copy(out=y_sb[:, e * C : (e + 1) * C], in_=y_ps[:])
+                mm_w(e, u, y_ps[:, half(u)], u == 0)
+            mm_wb(e, y_ps[:], slice(0, C))
+            nc.scalar.copy(out=y_sb[:, e * C : (e + 1) * C], in_=y_ps[:])
 
-        for e in range(E):
-            for s in range(PASSES):
-                step_wa(e, s)
-                if e == 0:
-                    gather_words(1, s, "wa_raw%d_%d" % (e, s))
-                if e > 0 and s == 0:
-                    hidden(e - 1)
-
-        hidden(last)
-        for e in wb_order:
-            cast_wb(e, e == wb_order[-1])
-            quant_wb(e)
-        y_last = [ypsum.tile([P, HALF], F32, name="y_ps%d" % last), hpsum.tile([P, HALF], F32, name="h_ps0")]
-        for u in (1, 0):
-            mm_w(last, u, y_last[u][:], True, False)
-        for u in (1, 0):
-            mm_wb(last, y_last[u][:], slice(u * HALF, (u + 1) * HALF), False, True)
-        nc.vector.tensor_copy(out=y_sb[:, last * C + HALF :], in_=y_last[1][:])
-        nc.scalar.copy(out=y_sb[:, last * C : last * C + HALF], in_=y_last[0][:])
-        for e in range(last):
-            finish(e, e == wb_order[-1])
-
-        parts = {}
+        spans = [slice(0, T - TAIL), slice(T - TAIL, T)]
+        gated = {}
 
         def fetch(b, r):
-            lst = pos_sb[r][:, spans[b].start // LIST : spans[b].stop // LIST]
-            parts[b, r] = kept([P, spans[b].stop - spans[b].start], F32, "part%d_%d" % (b, r))
-            nc.vector.tensor_tensor(parts[b, r][:], y_sb[:].indirect(lst), gate_sb[b][:, r, :], ALU.mult)
+            span = spans[b]
+            gated[b, r] = kept([P, span.stop - span.start], F32, "part%d_%d" % (b, r))
+            entries = pos_sb[r][:, span.start // LIST_ROWS : span.stop // LIST_ROWS]
+            nc.vector.tensor_tensor(gated[b, r][:], y_sb[:].indirect(entries), gate_sb[r][:, span], ALU.mult)
 
         def combine(b):
-            res = kept([P, spans[b].stop - spans[b].start], F32, "res%d" % b)
-            nc.vector.tensor_tensor(res[:], parts[b, 0][:], parts[b, 1][:], ALU.add)
-            nc.sync.dma_start(out=out[:, spans[b]], in_=res[:])
+            span = spans[b]
+            res = kept([P, span.stop - span.start], F32, "res%d" % b)
+            nc.vector.tensor_tensor(res[:], gated[b, 0][:], gated[b, 1][:], ALU.add)
+            nc.sync.dma_start(out=out[:, span], in_=res[:])
 
         fetch(0, 0)
         fetch(0, 1)

@@ -31,6 +31,7 @@ MOVED_ROWS = 112
 RING = 6
 SCALAR_ALONE = 4
 VECTOR_WB = 2
+LAST_SHARE = 24
 TAIL = 128
 
 
@@ -60,7 +61,7 @@ def tile_moe_elr_relu_kernel(
         y_sb = kept([P, E * C], F32, "y_sb")
         gate_sb = [kept([P, T], F32, "gate%d" % r) for r in range(2)]
 
-        nc.vector.memset(xs[:].bitcast(I32), 0)
+        nc.gpsimd.memset(xs[:].bitcast(I32), 0)
         for s in range(PASSES):
             nc.vector.memset(xw[s][:, T:], 0)
         nc.vector.memset(ws[:].rearrange("p a n -> p (a n)").bitcast(I32), 0)
@@ -68,13 +69,31 @@ def tile_moe_elr_relu_kernel(
             nc.vector.memset(xs_moved[s][:].bitcast(I32), 0)
 
         nc.sync.dma_start(offs_sb[:], offs)
+        wa_raw, wb_raw, ww, raw_names = {}, {}, {}, {}
+        wa_passes = wa.rearrange("e (s p j) c -> p (e s) j c", p=P, j=PACK)
+        steps = [(e, s) for e in range(E) for s in range(PASSES)]
+
+        def raw_name(e, s):
+            return raw_names[e, s]
+
+        def load_wa(group):
+            first = group[0][0] * PASSES + group[0][1]
+            raw = kept([P, len(group), PACK, H], F32, "wa_raw%d" % first)
+            nc.sync.dma_start(out=raw[:], in_=wa_passes[:, first : first + len(group)])
+            for i, step in enumerate(group):
+                wa_raw[step] = raw[:, i]
+                raw_names[step] = "wa_raw%d" % first
+
         for s in range(PASSES):
             nc.sync.dma_start(out=xw[s][:, :T], in_=x_words[s].rearrange("p t d -> p (t d)").bitcast(I32))
-        for q in range(P // QUAD):
-            nc.scalar.dma_start(
-                out=xs[QUAD * q : QUAD * q + QUAD_ROWS * PASSES, :T].bitcast(I32),
-                in_=x_scales.bitcast(I32)[:, QUAD_ROWS * q : QUAD_ROWS * (q + 1), :],
-            )
+            load_wa(steps[s : s + 1])
+            if s == 0:
+                for q in range(P // QUAD):
+                    queue = nc.scalar if q % 2 == 0 else nc.sync
+                    queue.dma_start(
+                        out=xs[QUAD * q : QUAD * q + QUAD_ROWS * PASSES, :T].bitcast(I32),
+                        in_=x_scales.bitcast(I32)[:, QUAD_ROWS * q : QUAD_ROWS * (q + 1), :],
+                    )
 
         xg = {}
         pairs = range(E * C // PAIR)
@@ -90,6 +109,7 @@ def tile_moe_elr_relu_kernel(
 
         for s in range(PASSES):
             gather_words(0, s, "xg%d" % s)
+        gather_words(1, 0, "xg_late0")
 
         def load_ws(r):
             rows = w_scales.bitcast(I32).rearrange("e s (q r) w -> r q (e s) w", r=QUAD_ROWS)
@@ -101,19 +121,11 @@ def tile_moe_elr_relu_kernel(
                 out=xs_moved[s][0:MOVED_ROWS, :].bitcast(I32), in_=xsg[first : first + MOVED_ROWS, :].bitcast(I32)
             )
 
-        wa_raw, wb_raw, ww = {}, {}, {}
-
-        def raw_name(e, s):
-            return "wa_raw%d_%d" % (e, s)
-
-        def load_wa(e, s):
-            wa_raw[e, s] = kept([P, PACK, H], F32, raw_name(e, s))
-            rows = wa[e, PASS_ROWS * s : PASS_ROWS * (s + 1), :].rearrange("(p j) c -> p j c", j=PACK)
-            nc.sync.dma_start(out=wa_raw[e, s][:], in_=rows)
-
-        def load_wb(e):
-            wb_raw[e] = kept([P, PACK, N], F32, "wb_raw%d" % e)
-            nc.sync.dma_start(out=wb_raw[e][:], in_=wb[e].rearrange("(p j) c -> p j c", j=PACK))
+        def load_wb(lo, hi):
+            raw = kept([P, hi - lo, PACK, N], F32, "wb_raw%d" % lo)
+            nc.sync.dma_start(out=raw[:], in_=wb[lo:hi].rearrange("e (p j) c -> p e j c", j=PACK))
+            for e in range(lo, hi):
+                wb_raw[e] = raw[:, e - lo]
 
         def load_ww(lo, hi):
             fp4 = kept([P, (hi - lo) * PASSES, 2 * N], U8, "ww%d" % lo)
@@ -121,18 +133,19 @@ def tile_moe_elr_relu_kernel(
             for e in range(lo, hi):
                 ww[e] = fp4[:, (e - lo) * PASSES : (e - lo + 1) * PASSES, :]
 
-        steps = [(e, s) for e in range(E) for s in range(PASSES)]
-        for e, s in steps[:-1]:
-            load_wa(e, s)
+        for first in range(PASSES, 7, 2):
+            load_wa(steps[first : first + 2])
+        for first in range(7, E * PASSES - 1):
+            load_wa(steps[first : first + 1])
         move_plane(1)
-        load_wa(*steps[-1])
-        load_wb(0)
+        load_wa(steps[-1:])
+        load_wb(0, 1)
         move_plane(2)
         for r in range(QUAD_ROWS):
             load_ws(r)
         load_ww(0, LAST)
         for e in range(1, E):
-            load_wb(e)
+            load_wb(e, e + 1)
         load_ww(LAST, E)
         for r, pos in enumerate((pos1, pos2)):
             nc.sync.dma_start(pos_sb[r][:], pos)
@@ -144,9 +157,13 @@ def tile_moe_elr_relu_kernel(
         def round_wa(e, s):
             rounded = ring.tile([P, PACK * H], BF16, name="wa_bf", align_bytes=64)
             dst = rounded[:].rearrange("p (g v m j) -> p g m j v", g=2, v=2, j=PACK)
-            src = wa_raw[e, s][:].rearrange("p j (m g v) -> p g m j v", g=2, v=2)
+            src = wa_raw[e, s].rearrange("p j (m g v) -> p g m j v", g=2, v=2)
             if e * PASSES + s < SCALAR_ALONE:
                 nc.scalar.copy(out=dst, in_=src)
+            elif (e, s) == (LAST, PASSES - 1):
+                nc.vector.tensor_copy(out=dst[:, 0], in_=src[:, 0])
+                nc.vector.tensor_copy(out=dst[:, 1, :LAST_SHARE], in_=src[:, 1, :LAST_SHARE])
+                nc.scalar.copy(out=dst[:, 1, LAST_SHARE:], in_=src[:, 1, LAST_SHARE:])
             else:
                 nc.vector.tensor_copy(out=dst[:, 0], in_=src[:, 0])
                 nc.scalar.copy(out=dst[:, 1], in_=src[:, 1])
@@ -183,7 +200,7 @@ def tile_moe_elr_relu_kernel(
         def prepare_wb(e):
             rounded = kept([P, PACK * N], BF16, "wb_bf%d" % e)
             dst = rounded[:].rearrange("p (c n j) -> p c j n", n=4, j=PACK)
-            src = wb_raw[e][:].rearrange("p j (c n) -> p c j n", n=4)
+            src = wb_raw[e].rearrange("p j (c n) -> p c j n", n=4)
             if e >= E - VECTOR_WB:
                 nc.vector.tensor_copy(out=dst, in_=src)
             else:
@@ -198,8 +215,13 @@ def tile_moe_elr_relu_kernel(
             h_scales[e] = kept([P, C], U8, "h_scales%d" % e)
             by_slot = [h_ps[e, u][:].rearrange("p t n -> p n t") for u in range(2)]
             nc.scalar.activation(out=rounded[:, half(0), :], in_=by_slot[0], func=RELU)
-            nc.vector.tensor_scalar_max(out=rounded[:, half(1), :], in0=by_slot[1], scalar1=0.0)
-            for cols in [half(1), half(0)] if e == LAST else [slice(0, C)]:
+            quarters = [slice(0, HALF // 2), slice(HALF // 2, HALF)] if e == LAST else [slice(0, HALF)]
+            for part in quarters:
+                nc.vector.tensor_scalar_max(
+                    out=rounded[:, HALF + part.start : HALF + part.stop, :], in0=by_slot[1][:, part, :], scalar1=0.0
+                )
+            pieces = [slice(HALF, HALF + HALF // 2), half(0), slice(HALF + HALF // 2, C)] if e == LAST else [slice(0, C)]
+            for cols in pieces:
                 nc.vector.quantize_mx(
                     out=h_codes[e][:, cols].bitcast(FP8X4), scales=h_scales[e][:, cols],
                     in_=rounded[:, cols, :].rearrange("p n t -> p (n t)"),
@@ -226,7 +248,7 @@ def tile_moe_elr_relu_kernel(
 
         for e, s in steps:
             step_wa(e, s)
-            if e == 0:
+            if e == 0 and s > 0:
                 gather_words(1, s, raw_name(e, s))
             if e > 0 and s == 0:
                 hidden(e - 1, raw_name(e, s))
@@ -249,7 +271,7 @@ def tile_moe_elr_relu_kernel(
             mm_wb(e, y_ps[:], slice(0, C))
             nc.scalar.copy(out=y_sb[:, e * C : (e + 1) * C], in_=y_ps[:])
 
-        spans = [slice(0, T - TAIL), slice(T - TAIL, T)]
+        spans = [slice(0, T - 2 * TAIL), slice(T - 2 * TAIL, T - TAIL), slice(T - TAIL, T)]
         gated = {}
 
         def fetch(b, r):
@@ -268,5 +290,8 @@ def tile_moe_elr_relu_kernel(
         fetch(0, 1)
         fetch(1, 0)
         combine(0)
+        fetch(2, 0)
         fetch(1, 1)
+        fetch(2, 1)
         combine(1)
+        combine(2)

@@ -14,6 +14,7 @@ U8 = mybir.dt.uint8
 FP8X4 = mybir.dt.float8_e4m3fn_x4
 FP4X4 = mybir.dt.float4_e2m1fn_x4
 RELU = mybir.ActivationFunctionType.Relu
+COPY = mybir.ActivationFunctionType.Copy
 ALU = mybir.AluOpType
 
 P = 128
@@ -271,27 +272,20 @@ def tile_moe_elr_relu_kernel(
             mm_wb(e, y_ps[:], slice(0, C))
             nc.scalar.copy(out=y_sb[:, e * C : (e + 1) * C], in_=y_ps[:])
 
-        spans = [slice(0, T - 2 * TAIL), slice(T - 2 * TAIL, T - TAIL), slice(T - TAIL, T)]
-        gated = {}
+        first = kept([P, T], F32, "first")
+        second = [kept([P, T // 2], F32, "second%d" % b) for b in range(2)]
+        second_gated = kept([P, T], F32, "second_gated")
+        res = kept([P, T], F32, "res")
 
-        def fetch(b, r):
-            span = spans[b]
-            gated[b, r] = kept([P, span.stop - span.start], F32, "part%d_%d" % (b, r))
-            entries = pos_sb[r][:, span.start // LIST_ROWS : span.stop // LIST_ROWS]
-            nc.vector.tensor_tensor(gated[b, r][:], y_sb[:].indirect(entries), gate_sb[r][:, span], ALU.mult)
+        def entries(r, span):
+            return pos_sb[r][:, span.start // LIST_ROWS : span.stop // LIST_ROWS]
 
-        def combine(b):
-            span = spans[b]
-            res = kept([P, span.stop - span.start], F32, "res%d" % b)
-            nc.vector.tensor_tensor(res[:], gated[b, 0][:], gated[b, 1][:], ALU.add)
-            nc.sync.dma_start(out=out[:, span], in_=res[:])
-
-        fetch(0, 0)
-        fetch(0, 1)
-        fetch(1, 0)
-        combine(0)
-        fetch(2, 0)
-        fetch(1, 1)
-        fetch(2, 1)
-        combine(1)
-        combine(2)
+        halves = [slice(0, T // 2), slice(T // 2, T)]
+        for b, span in enumerate(halves):
+            nc.scalar.activation(second[b][:], y_sb[:].indirect(entries(1, span)), COPY)
+            nc.vector.tensor_tensor(first[:, span], y_sb[:].indirect(entries(0, span)), gate_sb[0][:, span], ALU.mult)
+        for b, span in enumerate(halves):
+            nc.vector.tensor_tensor(second_gated[:, span], second[b][:], gate_sb[1][:, span], ALU.mult)
+        for span in (slice(0, T - 2 * TAIL), slice(T - 2 * TAIL, T - TAIL), slice(T - TAIL, T)):
+            nc.vector.tensor_tensor(res[:, span], first[:, span], second_gated[:, span], ALU.add)
+            nc.sync.dma_start(out=out[:, span], in_=res[:, span])

@@ -32,6 +32,7 @@ MOVED_ROWS = 112
 RING = 6
 SCALAR_ALONE = 4
 VECTOR_WB = 2
+WB_SHARE = 18
 LAST_SHARE = 24
 TAIL = 128
 
@@ -69,7 +70,6 @@ def tile_moe_elr_relu_kernel(
         for s in range(1, PASSES):
             nc.vector.memset(xs_moved[s][:].bitcast(I32), 0)
 
-        nc.sync.dma_start(offs_sb[:], offs)
         wa_raw, wb_raw, ww, raw_names = {}, {}, {}, {}
         wa_passes = wa.rearrange("e (s p j) c -> p (e s) j c", p=P, j=PACK)
         steps = [(e, s) for e in range(E) for s in range(PASSES)]
@@ -85,16 +85,22 @@ def tile_moe_elr_relu_kernel(
                 wa_raw[step] = raw[:, i]
                 raw_names[step] = "wa_raw%d" % first
 
-        for s in range(PASSES):
+        def load_words(s):
             nc.sync.dma_start(out=xw[s][:, :T], in_=x_words[s].rearrange("p t d -> p (t d)").bitcast(I32))
-            load_wa(steps[s : s + 1])
-            if s == 0:
-                for q in range(P // QUAD):
-                    queue = nc.scalar if q % 2 == 0 else nc.sync
-                    queue.dma_start(
-                        out=xs[QUAD * q : QUAD * q + QUAD_ROWS * PASSES, :T].bitcast(I32),
-                        in_=x_scales.bitcast(I32)[:, QUAD_ROWS * q : QUAD_ROWS * (q + 1), :],
-                    )
+
+        load_words(0)
+        nc.sync.dma_start(offs_sb[:], offs)
+        load_wa(steps[0:1])
+        load_words(1)
+        for q in range(P // QUAD):
+            queue = nc.scalar if q % 2 == 0 else nc.sync
+            queue.dma_start(
+                out=xs[QUAD * q : QUAD * q + QUAD_ROWS * PASSES, :T].bitcast(I32),
+                in_=x_scales.bitcast(I32)[:, QUAD_ROWS * q : QUAD_ROWS * (q + 1), :],
+            )
+        load_wa(steps[1:2])
+        load_words(2)
+        load_wa(steps[2:3])
 
         xg = {}
         pairs = range(E * C // PAIR)
@@ -128,11 +134,13 @@ def tile_moe_elr_relu_kernel(
             for e in range(lo, hi):
                 wb_raw[e] = raw[:, e - lo]
 
-        def load_ww(lo, hi):
-            fp4 = kept([P, (hi - lo) * PASSES, 2 * N], U8, "ww%d" % lo)
-            nc.sync.dma_start(out=fp4[:].bitcast(I32), in_=w_words[lo:hi].bitcast(I32).rearrange("e s p w -> p (e s) w"))
-            for e in range(lo, hi):
-                ww[e] = fp4[:, (e - lo) * PASSES : (e - lo + 1) * PASSES, :]
+        def load_ww(group):
+            first = group[0][0] * PASSES + group[0][1]
+            fp4 = kept([P, len(group), 2 * N], U8, "ww%d" % first)
+            words = w_words.bitcast(I32).rearrange("e s p w -> p (e s) w")
+            nc.sync.dma_start(out=fp4[:].bitcast(I32), in_=words[:, first : first + len(group)])
+            for i, step in enumerate(group):
+                ww[step] = fp4[:, i]
 
         for first in range(PASSES, 7, 2):
             load_wa(steps[first : first + 2])
@@ -144,12 +152,14 @@ def tile_moe_elr_relu_kernel(
         move_plane(2)
         for r in range(QUAD_ROWS):
             load_ws(r)
-        load_ww(0, LAST)
+        load_ww(steps[: LAST * PASSES])
         for e in range(1, E):
             load_wb(e, e + 1)
-        load_ww(LAST, E)
+        load_ww(steps[LAST * PASSES : -1])
+        load_ww(steps[-1:])
         for r, pos in enumerate((pos1, pos2)):
             nc.sync.dma_start(pos_sb[r][:], pos)
+        for r in range(2):
             nc.sync.dma_start(out=gate_sb[r][:], in_=gate[r])
 
         h_ps = {}
@@ -202,7 +212,10 @@ def tile_moe_elr_relu_kernel(
             rounded = kept([P, PACK * N], BF16, "wb_bf%d" % e)
             dst = rounded[:].rearrange("p (c n j) -> p c j n", n=4, j=PACK)
             src = wb_raw[e].rearrange("p j (c n) -> p c j n", n=4)
-            if e >= E - VECTOR_WB:
+            if e == LAST:
+                nc.vector.tensor_copy(out=dst[:, :WB_SHARE], in_=src[:, :WB_SHARE])
+                nc.scalar.copy(out=dst[:, WB_SHARE:], in_=src[:, WB_SHARE:])
+            elif e >= E - VECTOR_WB:
                 nc.vector.tensor_copy(out=dst, in_=src)
             else:
                 nc.scalar.copy(out=dst, in_=src)
@@ -228,15 +241,15 @@ def tile_moe_elr_relu_kernel(
                     in_=rounded[:, cols, :].rearrange("p n t -> p (n t)"),
                 )
 
-        def mm_w(e, u, target, start):
-            slots = slice(e * C + u * HALF, e * C + (u + 1) * HALF)
-            for s in range(PASSES):
+        def mm_w(e, cols, target, passes):
+            slots = slice(e * C + cols.start, e * C + cols.stop)
+            for s in passes:
                 plane = xsg if s == 0 else xs_moved[s]
                 nc.tensor.matmul_mx(
                     out=target,
-                    lhsT=ww[e][:, s, :].bitcast(FP4X4), lhsT_scale=ws[:, e * PASSES + s, :],
-                    rhs=xg[e, s][:, half(u)].bitcast(FP8X4), rhs_scale=plane[:, slots],
-                    start=(start and s == 0), stop=False,
+                    lhsT=ww[e, s].bitcast(FP4X4), lhsT_scale=ws[:, e * PASSES + s, :],
+                    rhs=xg[e, s][:, cols].bitcast(FP8X4), rhs_scale=plane[:, slots],
+                    start=(s == 0), stop=False,
                 )
 
         def mm_wb(e, target, cols):
@@ -259,16 +272,16 @@ def tile_moe_elr_relu_kernel(
             prepare_wb(e)
 
         y_last = [ypsum.tile([P, HALF], F32, name="y_ps%d" % LAST), hpsum.tile([P, HALF], F32, name="h_ps0")]
-        for u in (1, 0):
-            mm_w(LAST, u, y_last[u][:], True)
+        for passes in (range(PASSES - 1), range(PASSES - 1, PASSES)):
+            for u in (1, 0):
+                mm_w(LAST, half(u), y_last[u][:], passes)
         for u in (1, 0):
             mm_wb(LAST, y_last[u][:], half(u))
         nc.vector.tensor_copy(out=y_sb[:, LAST * C + HALF :], in_=y_last[1][:])
         nc.scalar.copy(out=y_sb[:, LAST * C : LAST * C + HALF], in_=y_last[0][:])
         for e in range(LAST):
             y_ps = ypsum.tile([P, C], F32, name="y_ps%d" % e)
-            for u in range(2):
-                mm_w(e, u, y_ps[:, half(u)], u == 0)
+            mm_w(e, slice(0, C), y_ps[:], range(PASSES))
             mm_wb(e, y_ps[:], slice(0, C))
             nc.scalar.copy(out=y_sb[:, e * C : (e + 1) * C], in_=y_ps[:])
 

@@ -30,7 +30,7 @@ PAIR = 2 * C
 WINDOW = T + 192
 MOVED_ROWS = 112
 RING = 6
-SCALAR_ALONE = 4
+SCALAR_ALONE = 6
 VECTOR_WB = 2
 WB_SHARE = 18
 LAST_SHARE = 24
@@ -142,9 +142,7 @@ def tile_moe_elr_relu_kernel(
             for i, step in enumerate(group):
                 ww[step] = fp4[:, i]
 
-        for first in range(PASSES, 7, 2):
-            load_wa(steps[first : first + 2])
-        for first in range(7, E * PASSES - 1):
+        for first in range(PASSES, E * PASSES - 1):
             load_wa(steps[first : first + 1])
         move_plane(1)
         load_wa(steps[-1:])

@@ -27,11 +27,11 @@ QUAD = 32
 QUAD_ROWS = 4
 LIST_ROWS = 16
 PAIR = 2 * C
-WINDOW = T + 192
+SPARE = 192
 MOVED_ROWS = 112
 RING = 6
-SCALAR_ALONE = 6
-VECTOR_WB = 2
+SCALAR_ALONE = 3
+VECTOR_SHARE = 48
 WB_SHARE = 18
 LAST_SHARE = 24
 TAIL = 128
@@ -44,8 +44,7 @@ def tile_moe_elr_relu_kernel(
     with ExitStack() as ctx:
         keep = ctx.enter_context(tc.tile_pool(name="keep", bufs=1))
         ring = ctx.enter_context(tc.tile_pool(name="ring", bufs=RING))
-        hpsum = ctx.enter_context(tc.psum_pool(name="hpsum", bufs=2))
-        ypsum = ctx.enter_context(tc.psum_pool(name="ypsum", bufs=1))
+        psum = ctx.enter_context(tc.psum_pool(name="psum", bufs=1))
 
         def kept(shape, dtype, name):
             return keep.tile(shape, dtype, name=name, align_bytes=64)
@@ -53,10 +52,14 @@ def tile_moe_elr_relu_kernel(
         def half(u):
             return slice(u * HALF, (u + 1) * HALF)
 
+        def bank_name(e, u):
+            return "bank%d_%d" % (e, u)
+
         offs_sb = keep.tile([P, E * C // LIST_ROWS], U16, name="offs_sb")
         pos_sb = [keep.tile([P, T // LIST_ROWS], U16, name="pos%d_sb" % r) for r in range(2)]
-        xw = [kept([P, WINDOW], I32, "xw%d" % s) for s in range(PASSES)]
-        xs = kept([P, WINDOW], U8, "xs")
+        xw_first = kept([P, T + SPARE], I32, "xw_first")
+        xw_later = kept([P, (PASSES - 1) * T + SPARE], I32, "xw_later")
+        xs = kept([P, T + SPARE], U8, "xs")
         xsg = kept([P, E * C], U8, "xsg")
         xs_moved = {s: kept([P, E * C], U8, "xs_low%d" % s) for s in range(1, PASSES)}
         ws = kept([P, E * PASSES, N], U8, "ws")
@@ -64,59 +67,25 @@ def tile_moe_elr_relu_kernel(
         gate_sb = [kept([P, T], F32, "gate%d" % r) for r in range(2)]
 
         nc.gpsimd.memset(xs[:].bitcast(I32), 0)
-        for s in range(PASSES):
-            nc.vector.memset(xw[s][:, T:], 0)
+        nc.vector.memset(xw_first[:, T:], 0)
+        nc.vector.memset(xw_later[:, (PASSES - 1) * T :], 0)
         nc.vector.memset(ws[:].rearrange("p a n -> p (a n)").bitcast(I32), 0)
         for s in range(1, PASSES):
             nc.vector.memset(xs_moved[s][:].bitcast(I32), 0)
 
-        wa_raw, wb_raw, ww, raw_names = {}, {}, {}, {}
-        wa_passes = wa.rearrange("e (s p j) c -> p (e s) j c", p=P, j=PACK)
+        wa_raw, raw_name, wb_raw, ww = {}, {}, {}, {}
+        wa_rows = wa.rearrange("e (s p j) c -> p (e s) (j c)", p=P, j=PACK)
+        words = x_words.rearrange("s p t d -> p s (t d)").bitcast(I32)
         steps = [(e, s) for e in range(E) for s in range(PASSES)]
 
-        def raw_name(e, s):
-            return raw_names[e, s]
-
         def load_wa(group):
-            first = group[0][0] * PASSES + group[0][1]
-            raw = kept([P, len(group), PACK, H], F32, "wa_raw%d" % first)
-            nc.sync.dma_start(out=raw[:], in_=wa_passes[:, first : first + len(group)])
+            first = steps.index(group[0])
+            name = "wa_raw%d" % first
+            raw = kept([P, len(group), PACK * H], F32, name)
+            nc.sync.dma_start(out=raw[:], in_=wa_rows[:, first : first + len(group)])
             for i, step in enumerate(group):
                 wa_raw[step] = raw[:, i]
-                raw_names[step] = "wa_raw%d" % first
-
-        def load_words(s):
-            nc.sync.dma_start(out=xw[s][:, :T], in_=x_words[s].rearrange("p t d -> p (t d)").bitcast(I32))
-
-        load_words(0)
-        nc.sync.dma_start(offs_sb[:], offs)
-        load_wa(steps[0:1])
-        load_words(1)
-        for q in range(P // QUAD):
-            queue = nc.scalar if q % 2 == 0 else nc.sync
-            queue.dma_start(
-                out=xs[QUAD * q : QUAD * q + QUAD_ROWS * PASSES, :T].bitcast(I32),
-                in_=x_scales.bitcast(I32)[:, QUAD_ROWS * q : QUAD_ROWS * (q + 1), :],
-            )
-        load_wa(steps[1:2])
-        load_words(2)
-        load_wa(steps[2:3])
-
-        xg = {}
-        pairs = range(E * C // PAIR)
-        pair_list = [offs_sb[:, b * (PAIR // LIST_ROWS) : (b + 1) * (PAIR // LIST_ROWS)] for b in pairs]
-        for b in pairs:
-            nc.vector.tensor_copy(xsg[:, b * PAIR : (b + 1) * PAIR], xs[:].indirect(pair_list[b]))
-
-        def gather_words(b, s, name):
-            gathered = kept([P, PAIR], U32, name)
-            nc.vector.tensor_copy(gathered[:], xw[s][:].bitcast(U32).indirect(pair_list[b]))
-            for i in range(2):
-                xg[2 * b + i, s] = gathered[:, i * C : (i + 1) * C]
-
-        for s in range(PASSES):
-            gather_words(0, s, "xg%d" % s)
-        gather_words(1, 0, "xg_late0")
+                raw_name[step] = name
 
         def load_ws(r):
             rows = w_scales.bitcast(I32).rearrange("e s (q r) w -> r q (e s) w", r=QUAD_ROWS)
@@ -129,32 +98,62 @@ def tile_moe_elr_relu_kernel(
             )
 
         def load_wb(lo, hi):
-            raw = kept([P, hi - lo, PACK, N], F32, "wb_raw%d" % lo)
-            nc.sync.dma_start(out=raw[:], in_=wb[lo:hi].rearrange("e (p j) c -> p e j c", j=PACK))
+            raw = kept([P, hi - lo, PACK * N], F32, "wb_raw%d" % lo)
+            nc.sync.dma_start(out=raw[:], in_=wb[lo:hi].rearrange("e (p j) c -> p e (j c)", j=PACK))
             for e in range(lo, hi):
                 wb_raw[e] = raw[:, e - lo]
 
-        def load_ww(group):
-            first = group[0][0] * PASSES + group[0][1]
-            fp4 = kept([P, len(group), 2 * N], U8, "ww%d" % first)
-            words = w_words.bitcast(I32).rearrange("e s p w -> p (e s) w")
-            nc.sync.dma_start(out=fp4[:].bitcast(I32), in_=words[:, first : first + len(group)])
-            for i, step in enumerate(group):
-                ww[step] = fp4[:, i]
+        def load_ww(lo, hi):
+            fp4 = kept([P, (hi - lo) * PASSES, 2 * N], U8, "ww%d" % lo)
+            rows = w_words.bitcast(I32).rearrange("e s p w -> p (e s) w")
+            nc.sync.dma_start(out=fp4[:].bitcast(I32), in_=rows[:, lo * PASSES : hi * PASSES])
+            for e in range(lo, hi):
+                for s in range(PASSES):
+                    ww[e, s] = fp4[:, (e - lo) * PASSES + s]
 
-        for first in range(PASSES, E * PASSES - 1):
-            load_wa(steps[first : first + 1])
-        move_plane(1)
-        load_wa(steps[-1:])
+        nc.sync.dma_start(out=xw_first[:, :T], in_=words[:, 0])
+        nc.sync.dma_start(offs_sb[:], offs)
+        load_wa(steps[0:1])
+        for q in range(P // QUAD):
+            queue = nc.scalar if q % 2 == 0 else nc.sync
+            queue.dma_start(
+                out=xs[QUAD * q : QUAD * q + QUAD_ROWS * PASSES, :T].bitcast(I32),
+                in_=x_scales.bitcast(I32)[:, QUAD_ROWS * q : QUAD_ROWS * (q + 1), :],
+            )
+        nc.sync.dma_start(
+            out=xw_later[:, : (PASSES - 1) * T].rearrange("p (s t) -> p s t", t=T), in_=words[:, 1:]
+        )
+        load_wa(steps[1:3])
+
+        xg = {}
+        pairs = range(E * C // PAIR)
+        pair_list = [offs_sb[:, b * (PAIR // LIST_ROWS) : (b + 1) * (PAIR // LIST_ROWS)] for b in pairs]
+
+        def gather_words(b, s):
+            window = xw_first[:] if s == 0 else xw_later[:, (s - 1) * T : s * T + SPARE]
+            gathered = kept([P, PAIR], U32, "xg%d_%d" % (b, s))
+            nc.vector.tensor_copy(gathered[:], window.bitcast(U32).indirect(pair_list[b]))
+            for i in range(2):
+                xg[2 * b + i, s] = gathered[:, i * C : (i + 1) * C]
+
+        for b in pairs:
+            gather_words(b, 0)
+        for b in pairs:
+            nc.vector.tensor_copy(xsg[:, b * PAIR : (b + 1) * PAIR], xs[:].indirect(pair_list[b]))
+
+        load_wa(steps[3:5])
+        for i in range(5, E * PASSES):
+            if i == E * PASSES - 1:
+                move_plane(1)
+            load_wa(steps[i : i + 1])
         load_wb(0, 1)
         move_plane(2)
         for r in range(QUAD_ROWS):
             load_ws(r)
-        load_ww(steps[: LAST * PASSES])
+        load_ww(0, LAST)
         for e in range(1, E):
             load_wb(e, e + 1)
-        load_ww(steps[LAST * PASSES : -1])
-        load_ww(steps[-1:])
+        load_ww(LAST, E)
         for r, pos in enumerate((pos1, pos2)):
             nc.sync.dma_start(pos_sb[r][:], pos)
         for r in range(2):
@@ -163,25 +162,25 @@ def tile_moe_elr_relu_kernel(
         h_ps = {}
         wb_codes, wb_scales, h_codes, h_scales = {}, {}, {}, {}
 
-        def round_wa(e, s):
+        def round_wa(step):
             rounded = ring.tile([P, PACK * H], BF16, name="wa_bf", align_bytes=64)
             dst = rounded[:].rearrange("p (g v m j) -> p g m j v", g=2, v=2, j=PACK)
-            src = wa_raw[e, s].rearrange("p j (m g v) -> p g m j v", g=2, v=2)
-            if e * PASSES + s < SCALAR_ALONE:
+            src = wa_raw[step].rearrange("p (j m g v) -> p g m j v", g=2, v=2, j=PACK)
+            if steps.index(step) < SCALAR_ALONE:
                 nc.scalar.copy(out=dst, in_=src)
-            elif (e, s) == (LAST, PASSES - 1):
+            elif step == steps[-1]:
                 nc.vector.tensor_copy(out=dst[:, 0], in_=src[:, 0])
                 nc.vector.tensor_copy(out=dst[:, 1, :LAST_SHARE], in_=src[:, 1, :LAST_SHARE])
                 nc.scalar.copy(out=dst[:, 1, LAST_SHARE:], in_=src[:, 1, LAST_SHARE:])
             else:
-                nc.vector.tensor_copy(out=dst[:, 0], in_=src[:, 0])
-                nc.scalar.copy(out=dst[:, 1], in_=src[:, 1])
+                nc.vector.tensor_copy(out=dst[:, :, :VECTOR_SHARE], in_=src[:, :, :VECTOR_SHARE])
+                nc.scalar.copy(out=dst[:, :, VECTOR_SHARE:], in_=src[:, :, VECTOR_SHARE:])
             return rounded
 
         def mm_wa(e, s, codes, scales, outputs):
             for u in (1, 0):
                 if s == 0:
-                    h_ps[e, u] = hpsum.tile([P, PACK, HALF], F32, name="h_ps%d" % u)
+                    h_ps[e, u] = psum.tile([P, PACK, HALF], F32, name=bank_name(e, u))
                 for t in outputs:
                     m = slice(t * P, (t + 1) * P)
                     nc.tensor.matmul_mx(
@@ -193,9 +192,13 @@ def tile_moe_elr_relu_kernel(
                     )
 
         def step_wa(e, s):
-            rounded = round_wa(e, s)
-            codes = ring.tile([P, H], U32, name="wa_codes", align_bytes=64)
-            scales = ring.tile([P, H], U8, name="wa_scales", align_bytes=64)
+            rounded = round_wa((e, s))
+            if (e, s) == steps[-1]:
+                codes = kept([P, H], U32, "last_codes")
+                scales = kept([P, H], U8, "last_scales")
+            else:
+                codes = ring.tile([P, H], U32, name="wa_codes", align_bytes=64)
+                scales = ring.tile([P, H], U8, name="wa_scales", align_bytes=64)
             pieces = 2 if (e, s) == steps[-1] else 1
             width = H // pieces
             for g in range(pieces):
@@ -206,20 +209,19 @@ def tile_moe_elr_relu_kernel(
                 )
                 mm_wa(e, s, codes, scales, range(g * PACK // pieces, (g + 1) * PACK // pieces))
 
-        def prepare_wb(e):
-            rounded = kept([P, PACK * N], BF16, "wb_bf%d" % e)
-            dst = rounded[:].rearrange("p (c n j) -> p c j n", n=4, j=PACK)
-            src = wb_raw[e].rearrange("p j (c n) -> p c j n", n=4)
+        def prepare_wb(e, rounded):
+            dst = rounded.rearrange("p (c n j) -> p c j n", n=4, j=PACK)
+            src = wb_raw[e].rearrange("p (j c n) -> p c j n", n=4, j=PACK)
             if e == LAST:
                 nc.vector.tensor_copy(out=dst[:, :WB_SHARE], in_=src[:, :WB_SHARE])
                 nc.scalar.copy(out=dst[:, WB_SHARE:], in_=src[:, WB_SHARE:])
-            elif e >= E - VECTOR_WB:
+            elif e == LAST - 1:
                 nc.vector.tensor_copy(out=dst, in_=src)
             else:
                 nc.scalar.copy(out=dst, in_=src)
             wb_codes[e] = kept([P, N], U32, "wb_codes%d" % e)
             wb_scales[e] = kept([P, N], U8, "wb_scales%d" % e)
-            nc.vector.quantize_mx(out=wb_codes[e][:].bitcast(FP8X4), scales=wb_scales[e][:], in_=rounded[:])
+            nc.vector.quantize_mx(out=wb_codes[e][:].bitcast(FP8X4), scales=wb_scales[e][:], in_=rounded)
 
         def hidden(e, name):
             rounded = kept([P, C, PACK], BF16, name)
@@ -239,49 +241,58 @@ def tile_moe_elr_relu_kernel(
                     in_=rounded[:, cols, :].rearrange("p n t -> p (n t)"),
                 )
 
-        def mm_w(e, cols, target, passes):
+        def mm_w(e, cols, target, opens):
             slots = slice(e * C + cols.start, e * C + cols.stop)
-            for s in passes:
+            for s in range(PASSES):
                 plane = xsg if s == 0 else xs_moved[s]
                 nc.tensor.matmul_mx(
                     out=target,
                     lhsT=ww[e, s].bitcast(FP4X4), lhsT_scale=ws[:, e * PASSES + s, :],
                     rhs=xg[e, s][:, cols].bitcast(FP8X4), rhs_scale=plane[:, slots],
-                    start=(s == 0), stop=False,
+                    start=(opens and s == 0), stop=(not opens and s == PASSES - 1),
                 )
 
-        def mm_wb(e, target, cols):
+        def mm_wb(e, target, cols, opens):
             nc.tensor.matmul_mx(
                 out=target,
                 lhsT=wb_codes[e][:].bitcast(FP8X4), lhsT_scale=wb_scales[e][:],
                 rhs=h_codes[e][:, cols].bitcast(FP8X4), rhs_scale=h_scales[e][:, cols],
-                start=False, stop=True,
+                start=opens, stop=not opens,
             )
 
-        for e, s in steps:
+        whole = slice(0, C)
+        y_ps = {}
+
+        def open_y(e):
+            y_ps[e] = psum.tile([P, C], F32, name=bank_name(e, 0))
+            mm_w(e, whole, y_ps[e][:], True)
+
+        def close_y(e):
+            mm_wb(e, y_ps[e][:], whole, False)
+            nc.scalar.copy(out=y_sb[:, e * C : (e + 1) * C], in_=y_ps[e][:])
+
+        for i, (e, s) in enumerate(steps):
             step_wa(e, s)
-            if e == 0 and s > 0:
-                gather_words(1, s, raw_name(e, s))
-            if e > 0 and s == 0:
-                hidden(e - 1, raw_name(e, s))
+            if i == 0:
+                for later in range(1, PASSES):
+                    for b in pairs:
+                        gather_words(b, later)
+            if e > 0 and s == (0 if e == LAST else 1):
+                hidden(e - 1, raw_name[e, s])
 
         hidden(LAST, "h_bf")
         for e in range(E):
-            prepare_wb(e)
-
-        y_last = [ypsum.tile([P, HALF], F32, name="y_ps%d" % LAST), hpsum.tile([P, HALF], F32, name="h_ps0")]
-        for passes in (range(PASSES - 1), range(PASSES - 1, PASSES)):
-            for u in (1, 0):
-                mm_w(LAST, half(u), y_last[u][:], passes)
+            prepare_wb(e, kept([P, PACK * N], BF16, "wb_bf%d" % e)[:])
+        y_last = [psum.tile([P, HALF], F32, name=bank_name(u, 1)) for u in range(2)]
         for u in (1, 0):
-            mm_wb(LAST, y_last[u][:], half(u))
+            mm_w(LAST, half(u), y_last[u][:], True)
+        for u in (1, 0):
+            mm_wb(LAST, y_last[u][:], half(u), False)
         nc.vector.tensor_copy(out=y_sb[:, LAST * C + HALF :], in_=y_last[1][:])
         nc.scalar.copy(out=y_sb[:, LAST * C : LAST * C + HALF], in_=y_last[0][:])
         for e in range(LAST):
-            y_ps = ypsum.tile([P, C], F32, name="y_ps%d" % e)
-            mm_w(e, slice(0, C), y_ps[:], range(PASSES))
-            mm_wb(e, y_ps[:], slice(0, C))
-            nc.scalar.copy(out=y_sb[:, e * C : (e + 1) * C], in_=y_ps[:])
+            open_y(e)
+            close_y(e)
 
         first = kept([P, T], F32, "first")
         second = [kept([P, T // 2], F32, "second%d" % b) for b in range(2)]
@@ -294,7 +305,7 @@ def tile_moe_elr_relu_kernel(
         halves = [slice(0, T // 2), slice(T // 2, T)]
         for b, span in enumerate(halves):
             nc.scalar.activation(second[b][:], y_sb[:].indirect(entries(1, span)), COPY)
-            nc.vector.tensor_tensor(first[:, span], y_sb[:].indirect(entries(0, span)), gate_sb[0][:, span], ALU.mult)
+        nc.vector.tensor_tensor(first[:], y_sb[:].indirect(pos_sb[0][:]), gate_sb[0][:], ALU.mult)
         for b, span in enumerate(halves):
             nc.vector.tensor_tensor(second_gated[:, span], second[b][:], gate_sb[1][:, span], ALU.mult)
         for span in (slice(0, T - 2 * TAIL), slice(T - 2 * TAIL, T - TAIL), slice(T - TAIL, T)):

@@ -28,12 +28,12 @@ QUAD_ROWS = 4
 LIST_ROWS = 16
 PAIR = 2 * C
 SPARE = 192
-MOVED_ROWS = 112
-RING = 6
-SCALAR_ALONE = 3
-VECTOR_SHARE = 48
+RING = 7
+SCALAR_ALONE = 7
+VECTOR_SHARE = 68
 WB_SHARE = 18
 LAST_SHARE = 24
+WORDS_AT = 4
 TAIL = 128
 
 
@@ -59,19 +59,15 @@ def tile_moe_elr_relu_kernel(
         pos_sb = [keep.tile([P, T // LIST_ROWS], U16, name="pos%d_sb" % r) for r in range(2)]
         xw_first = kept([P, T + SPARE], I32, "xw_first")
         xw_later = kept([P, (PASSES - 1) * T + SPARE], I32, "xw_later")
-        xs = kept([P, T + SPARE], U8, "xs")
-        xsg = kept([P, E * C], U8, "xsg")
-        xs_moved = {s: kept([P, E * C], U8, "xs_low%d" % s) for s in range(1, PASSES)}
+        xs = kept([P, PASSES * T + SPARE], U8, "xs")
         ws = kept([P, E * PASSES, N], U8, "ws")
         y_sb = kept([P, E * C], F32, "y_sb")
         gate_sb = [kept([P, T], F32, "gate%d" % r) for r in range(2)]
 
-        nc.gpsimd.memset(xs[:].bitcast(I32), 0)
+        nc.vector.memset(xs[:].bitcast(I32), 0)
         nc.vector.memset(xw_first[:, T:], 0)
         nc.vector.memset(xw_later[:, (PASSES - 1) * T :], 0)
         nc.vector.memset(ws[:].rearrange("p a n -> p (a n)").bitcast(I32), 0)
-        for s in range(1, PASSES):
-            nc.vector.memset(xs_moved[s][:].bitcast(I32), 0)
 
         wa_raw, raw_name, wb_raw, ww = {}, {}, {}, {}
         wa_rows = wa.rearrange("e (s p j) c -> p (e s) (j c)", p=P, j=PACK)
@@ -91,12 +87,6 @@ def tile_moe_elr_relu_kernel(
             rows = w_scales.bitcast(I32).rearrange("e s (q r) w -> r q (e s) w", r=QUAD_ROWS)
             nc.sync.dma_start(out=ws[r:P:QUAD, :, :].bitcast(I32), in_=rows[r])
 
-        def move_plane(s):
-            first = QUAD_ROWS * s
-            nc.sync.dma_start(
-                out=xs_moved[s][0:MOVED_ROWS, :].bitcast(I32), in_=xsg[first : first + MOVED_ROWS, :].bitcast(I32)
-            )
-
         def load_wb(lo, hi):
             raw = kept([P, hi - lo, PACK * N], F32, "wb_raw%d" % lo)
             nc.sync.dma_start(out=raw[:], in_=wb[lo:hi].rearrange("e (p j) c -> p e (j c)", j=PACK))
@@ -114,40 +104,45 @@ def tile_moe_elr_relu_kernel(
         nc.sync.dma_start(out=xw_first[:, :T], in_=words[:, 0])
         nc.sync.dma_start(offs_sb[:], offs)
         load_wa(steps[0:1])
-        for q in range(P // QUAD):
-            queue = nc.scalar if q % 2 == 0 else nc.sync
+        scale_rows = x_scales.bitcast(I32).rearrange("s (q r) w -> r q s w", r=QUAD_ROWS)
+        for r in range(QUAD_ROWS):
+            queue = nc.scalar if r % 2 == 0 else nc.sync
             queue.dma_start(
-                out=xs[QUAD * q : QUAD * q + QUAD_ROWS * PASSES, :T].bitcast(I32),
-                in_=x_scales.bitcast(I32)[:, QUAD_ROWS * q : QUAD_ROWS * (q + 1), :],
+                out=xs[r:P:QUAD, : PASSES * T].bitcast(I32).rearrange("p (s w) -> p s w", s=PASSES), in_=scale_rows[r]
             )
+        for i in range(1, WORDS_AT):
+            load_wa(steps[i : i + 1])
         nc.sync.dma_start(
             out=xw_later[:, : (PASSES - 1) * T].rearrange("p (s t) -> p s t", t=T), in_=words[:, 1:]
         )
-        load_wa(steps[1:3])
 
-        xg = {}
+        xg, xsg = {}, {}
         pairs = range(E * C // PAIR)
         pair_list = [offs_sb[:, b * (PAIR // LIST_ROWS) : (b + 1) * (PAIR // LIST_ROWS)] for b in pairs]
 
-        def gather_words(b, s):
+        def gather_words(b, s, name):
             window = xw_first[:] if s == 0 else xw_later[:, (s - 1) * T : s * T + SPARE]
-            gathered = kept([P, PAIR], U32, "xg%d_%d" % (b, s))
+            gathered = kept([P, PAIR], U32, name)
             nc.vector.tensor_copy(gathered[:], window.bitcast(U32).indirect(pair_list[b]))
             for i in range(2):
                 xg[2 * b + i, s] = gathered[:, i * C : (i + 1) * C]
 
         for b in pairs:
-            gather_words(b, 0)
-        for b in pairs:
-            nc.vector.tensor_copy(xsg[:, b * PAIR : (b + 1) * PAIR], xs[:].indirect(pair_list[b]))
+            gather_words(b, 0, "xg%d_0" % b)
 
-        load_wa(steps[3:5])
-        for i in range(5, E * PASSES):
-            if i == E * PASSES - 1:
-                move_plane(1)
+        def gather_bytes(b, s, name):
+            gathered = kept([P, PAIR], U8, name)
+            nc.vector.tensor_copy(gathered[:], xs[:, s * T : (s + 1) * T + SPARE].indirect(pair_list[b]))
+            for i in range(2):
+                xsg[2 * b + i, s] = gathered[:, i * C : (i + 1) * C]
+
+        for b in pairs:
+            for s in range(PASSES):
+                gather_bytes(b, s, "xsg%d_%d" % (b, s))
+
+        for i in range(WORDS_AT, E * PASSES):
             load_wa(steps[i : i + 1])
         load_wb(0, 1)
-        move_plane(2)
         for r in range(QUAD_ROWS):
             load_ws(r)
         load_ww(0, LAST)
@@ -187,7 +182,7 @@ def tile_moe_elr_relu_kernel(
                         out=h_ps[e, u][:, t, :],
                         lhsT=codes[:, m].bitcast(FP8X4), lhsT_scale=scales[:, m],
                         rhs=xg[e, s][:, half(u)].bitcast(FP8X4),
-                        rhs_scale=xsg[QUAD_ROWS * s :, e * C + u * HALF : e * C + (u + 1) * HALF],
+                        rhs_scale=xsg[e, s][:, half(u)],
                         start=(s == 0 and t == 0), stop=(s == PASSES - 1 and t == PACK - 1),
                     )
 
@@ -242,13 +237,11 @@ def tile_moe_elr_relu_kernel(
                 )
 
         def mm_w(e, cols, target, opens):
-            slots = slice(e * C + cols.start, e * C + cols.stop)
             for s in range(PASSES):
-                plane = xsg if s == 0 else xs_moved[s]
                 nc.tensor.matmul_mx(
                     out=target,
                     lhsT=ww[e, s].bitcast(FP4X4), lhsT_scale=ws[:, e * PASSES + s, :],
-                    rhs=xg[e, s][:, cols].bitcast(FP8X4), rhs_scale=plane[:, slots],
+                    rhs=xg[e, s][:, cols].bitcast(FP8X4), rhs_scale=xsg[e, s][:, cols],
                     start=(opens and s == 0), stop=(not opens and s == PASSES - 1),
                 )
 
@@ -261,6 +254,7 @@ def tile_moe_elr_relu_kernel(
             )
 
         whole = slice(0, C)
+        relu_after = {(1, 2): 0, (2, 1): 1, (3, 0): 2}
         y_ps = {}
 
         def open_y(e):
@@ -275,10 +269,11 @@ def tile_moe_elr_relu_kernel(
             step_wa(e, s)
             if i == 0:
                 for later in range(1, PASSES):
-                    for b in pairs:
-                        gather_words(b, later)
-            if e > 0 and s == (0 if e == LAST else 1):
-                hidden(e - 1, raw_name[e, s])
+                    gather_words(0, later, "xg0_%d" % later)
+            if i in (3, 4):
+                gather_words(1, i - 2, raw_name[e, s])
+            if (e, s) in relu_after:
+                hidden(relu_after[e, s], raw_name[e, s])
 
         hidden(LAST, "h_bf")
         for e in range(E):

@@ -31,7 +31,6 @@ SPARE = 192
 RING = 7
 SCALAR_ALONE = 7
 VECTOR_SHARE = 68
-WB_SHARE = 18
 LAST_SHARE = 24
 WORDS_AT = 4
 TAIL = 128
@@ -142,13 +141,13 @@ def tile_moe_elr_relu_kernel(
 
         for i in range(WORDS_AT, E * PASSES):
             load_wa(steps[i : i + 1])
-        load_wb(0, 1)
+        load_wb(0, 2)
         for r in range(QUAD_ROWS):
             load_ws(r)
-        load_ww(0, LAST)
-        for e in range(1, E):
+        load_ww(0, 2)
+        for e in range(2, E):
             load_wb(e, e + 1)
-        load_ww(LAST, E)
+            load_ww(e, e + 1)
         for r, pos in enumerate((pos1, pos2)):
             nc.sync.dma_start(pos_sb[r][:], pos)
         for r in range(2):
@@ -204,19 +203,21 @@ def tile_moe_elr_relu_kernel(
                 )
                 mm_wa(e, s, codes, scales, range(g * PACK // pieces, (g + 1) * PACK // pieces))
 
-        def prepare_wb(e, rounded):
+        def round_wb(e, rounded):
             dst = rounded.rearrange("p (c n j) -> p c j n", n=4, j=PACK)
             src = wb_raw[e].rearrange("p (j c n) -> p c j n", n=4, j=PACK)
-            if e == LAST:
-                nc.vector.tensor_copy(out=dst[:, :WB_SHARE], in_=src[:, :WB_SHARE])
-                nc.scalar.copy(out=dst[:, WB_SHARE:], in_=src[:, WB_SHARE:])
-            elif e == LAST - 1:
+            if e % 2 == 1:
                 nc.vector.tensor_copy(out=dst, in_=src)
             else:
                 nc.scalar.copy(out=dst, in_=src)
-            wb_codes[e] = kept([P, N], U32, "wb_codes%d" % e)
-            wb_scales[e] = kept([P, N], U8, "wb_scales%d" % e)
-            nc.vector.quantize_mx(out=wb_codes[e][:].bitcast(FP8X4), scales=wb_scales[e][:], in_=rounded)
+
+        def quantise_wb(lo, hi, rounded):
+            codes = kept([P, (hi - lo) * N], U32, "wb_codes%d" % lo)
+            scales = kept([P, (hi - lo) * N], U8, "wb_scales%d" % lo)
+            nc.vector.quantize_mx(out=codes[:].bitcast(FP8X4), scales=scales[:], in_=rounded)
+            for e in range(lo, hi):
+                wb_codes[e] = codes[:, (e - lo) * N : (e - lo + 1) * N]
+                wb_scales[e] = scales[:, (e - lo) * N : (e - lo + 1) * N]
 
         def hidden(e, name):
             rounded = kept([P, C, PACK], BF16, name)
@@ -248,7 +249,7 @@ def tile_moe_elr_relu_kernel(
         def mm_wb(e, target, cols, opens):
             nc.tensor.matmul_mx(
                 out=target,
-                lhsT=wb_codes[e][:].bitcast(FP8X4), lhsT_scale=wb_scales[e][:],
+                lhsT=wb_codes[e].bitcast(FP8X4), lhsT_scale=wb_scales[e],
                 rhs=h_codes[e][:, cols].bitcast(FP8X4), rhs_scale=h_scales[e][:, cols],
                 start=opens, stop=not opens,
             )
@@ -275,19 +276,28 @@ def tile_moe_elr_relu_kernel(
             if (e, s) in relu_after:
                 hidden(relu_after[e, s], raw_name[e, s])
 
+        early = kept([P, 2 * PACK * N], BF16, raw_name[steps[-1]])
+        for e in range(2):
+            round_wb(e, early[:, e * PACK * N : (e + 1) * PACK * N])
+        quantise_wb(0, 2, early[:])
         hidden(LAST, "h_bf")
-        for e in range(E):
-            prepare_wb(e, kept([P, PACK * N], BF16, "wb_bf%d" % e)[:])
+        late = {e: kept([P, PACK * N], BF16, name) for e, name in ((LAST - 1, "last_codes"), (LAST, "last_scales"))}
+        for e in late:
+            round_wb(e, late[e][:])
+        for e in late:
+            quantise_wb(e, e + 1, late[e][:])
+        for e in range(2):
+            open_y(e)
+            close_y(e)
+        open_y(LAST - 1)
         y_last = [psum.tile([P, HALF], F32, name=bank_name(u, 1)) for u in range(2)]
         for u in (1, 0):
             mm_w(LAST, half(u), y_last[u][:], True)
+        close_y(LAST - 1)
         for u in (1, 0):
             mm_wb(LAST, y_last[u][:], half(u), False)
         nc.vector.tensor_copy(out=y_sb[:, LAST * C + HALF :], in_=y_last[1][:])
         nc.scalar.copy(out=y_sb[:, LAST * C : LAST * C + HALF], in_=y_last[0][:])
-        for e in range(LAST):
-            open_y(e)
-            close_y(e)
 
         first = kept([P, T], F32, "first")
         second = [kept([P, T // 2], F32, "second%d" % b) for b in range(2)]

@@ -33,6 +33,7 @@ SCALAR_ALONE = 7
 VECTOR_SHARE = 68
 LAST_SHARE = 24
 WORDS_AT = 4
+ALIGN = 256
 TAIL = 128
 
 
@@ -46,7 +47,7 @@ def tile_moe_elr_relu_kernel(
         psum = ctx.enter_context(tc.psum_pool(name="psum", bufs=1))
 
         def kept(shape, dtype, name):
-            return keep.tile(shape, dtype, name=name, align_bytes=64)
+            return keep.tile(shape, dtype, name=name, align_bytes=ALIGN)
 
         def half(u):
             return slice(u * HALF, (u + 1) * HALF)
@@ -54,8 +55,8 @@ def tile_moe_elr_relu_kernel(
         def bank_name(e, u):
             return "bank%d_%d" % (e, u)
 
-        offs_sb = keep.tile([P, E * C // LIST_ROWS], U16, name="offs_sb")
-        pos_sb = [keep.tile([P, T // LIST_ROWS], U16, name="pos%d_sb" % r) for r in range(2)]
+        offs_sb = keep.tile([P, E * C // LIST_ROWS], U16, name="offs_sb", align_bytes=ALIGN)
+        pos_sb = [keep.tile([P, T // LIST_ROWS], U16, name="pos%d_sb" % r, align_bytes=ALIGN) for r in range(2)]
         xw_first = kept([P, T + SPARE], I32, "xw_first")
         xw_later = kept([P, (PASSES - 1) * T + SPARE], I32, "xw_later")
         xs = kept([P, PASSES * T + SPARE], U8, "xs")
@@ -157,7 +158,7 @@ def tile_moe_elr_relu_kernel(
         wb_codes, wb_scales, h_codes, h_scales = {}, {}, {}, {}
 
         def round_wa(step):
-            rounded = ring.tile([P, PACK * H], BF16, name="wa_bf", align_bytes=64)
+            rounded = ring.tile([P, PACK * H], BF16, name="wa_bf", align_bytes=ALIGN)
             dst = rounded[:].rearrange("p (g v m j) -> p g m j v", g=2, v=2, j=PACK)
             src = wa_raw[step].rearrange("p (j m g v) -> p g m j v", g=2, v=2, j=PACK)
             if steps.index(step) < SCALAR_ALONE:
@@ -191,8 +192,8 @@ def tile_moe_elr_relu_kernel(
                 codes = kept([P, H], U32, "last_codes")
                 scales = kept([P, H], U8, "last_scales")
             else:
-                codes = ring.tile([P, H], U32, name="wa_codes", align_bytes=64)
-                scales = ring.tile([P, H], U8, name="wa_scales", align_bytes=64)
+                codes = ring.tile([P, H], U32, name="wa_codes", align_bytes=ALIGN)
+                scales = ring.tile([P, H], U8, name="wa_scales", align_bytes=ALIGN)
             pieces = 2 if (e, s) == steps[-1] else 1
             width = H // pieces
             for g in range(pieces):

@@ -142,7 +142,8 @@ def tile_moe_elr_relu_kernel(
 
         for i in range(WORDS_AT, E * PASSES):
             load_wa(steps[i : i + 1])
-        load_wb(0, 2)
+        for e in range(2):
+            load_wb(e, e + 1)
         for r in range(QUAD_ROWS):
             load_ws(r)
         load_ww(0, 2)
@@ -280,8 +281,9 @@ def tile_moe_elr_relu_kernel(
         early = kept([P, 2 * PACK * N], BF16, raw_name[steps[-1]])
         for e in range(2):
             round_wb(e, early[:, e * PACK * N : (e + 1) * PACK * N])
-        quantise_wb(0, 2, early[:])
-        hidden(LAST, "h_bf")
+        for e in range(2):
+            quantise_wb(e, e + 1, early[:, e * PACK * N : (e + 1) * PACK * N])
+        hidden(LAST, "wb_raw1")
         late = {e: kept([P, PACK * N], BF16, name) for e, name in ((LAST - 1, "last_codes"), (LAST, "last_scales"))}
         for e in late:
             round_wb(e, late[e][:])

@@ -57,16 +57,16 @@ def tile_moe_elr_relu_kernel(
 
         offs_sb = keep.tile([P, E * C // LIST_ROWS], U16, name="offs_sb", align_bytes=ALIGN)
         pos_sb = [keep.tile([P, T // LIST_ROWS], U16, name="pos%d_sb" % r, align_bytes=ALIGN) for r in range(2)]
-        xw_first = kept([P, T + SPARE], I32, "xw_first")
-        xw_later = kept([P, (PASSES - 1) * T + SPARE], I32, "xw_later")
+        xw_first = kept([P, (PASSES - 1) * T + SPARE], I32, "xw_first")
+        xw_later = kept([P, T + SPARE], I32, "xw_later")
         xs = kept([P, PASSES * T + SPARE], U8, "xs")
         ws = kept([P, E * PASSES, N], U8, "ws")
         y_sb = kept([P, E * C], F32, "y_sb")
         gate_sb = [kept([P, T], F32, "gate%d" % r) for r in range(2)]
 
         nc.vector.memset(xs[:].bitcast(I32), 0)
-        nc.vector.memset(xw_first[:, T:], 0)
-        nc.vector.memset(xw_later[:, (PASSES - 1) * T :], 0)
+        nc.vector.memset(xw_first[:, (PASSES - 1) * T :], 0)
+        nc.vector.memset(xw_later[:, T:], 0)
         nc.vector.memset(ws[:].rearrange("p a n -> p (a n)").bitcast(I32), 0)
 
         wa_raw, raw_name, wb_raw, ww = {}, {}, {}, {}
@@ -101,7 +101,9 @@ def tile_moe_elr_relu_kernel(
                 for s in range(PASSES):
                     ww[e, s] = fp4[:, (e - lo) * PASSES + s]
 
-        nc.sync.dma_start(out=xw_first[:, :T], in_=words[:, 0])
+        nc.sync.dma_start(
+            out=xw_first[:, : (PASSES - 1) * T].rearrange("p (s t) -> p s t", t=T), in_=words[:, : PASSES - 1]
+        )
         nc.sync.dma_start(offs_sb[:], offs)
         load_wa(steps[0:1])
         scale_rows = x_scales.bitcast(I32).rearrange("s (q r) w -> r q s w", r=QUAD_ROWS)
@@ -112,16 +114,14 @@ def tile_moe_elr_relu_kernel(
             )
         for i in range(1, WORDS_AT):
             load_wa(steps[i : i + 1])
-        nc.sync.dma_start(
-            out=xw_later[:, : (PASSES - 1) * T].rearrange("p (s t) -> p s t", t=T), in_=words[:, 1:]
-        )
+        nc.sync.dma_start(out=xw_later[:, :T], in_=words[:, PASSES - 1])
 
         xg, xsg = {}, {}
         pairs = range(E * C // PAIR)
         pair_list = [offs_sb[:, b * (PAIR // LIST_ROWS) : (b + 1) * (PAIR // LIST_ROWS)] for b in pairs]
 
         def gather_words(b, s, name):
-            window = xw_first[:] if s == 0 else xw_later[:, (s - 1) * T : s * T + SPARE]
+            window = xw_later[:] if s == PASSES - 1 else xw_first[:, s * T : (s + 1) * T + SPARE]
             gathered = kept([P, PAIR], U32, name)
             nc.vector.tensor_copy(gathered[:], window.bitcast(U32).indirect(pair_list[b]))
             for i in range(2):

from contextlib import ExitStack

import concourse.mybir as mybir

K, T, E, C, H, N = 1536, 512, 4, 256, 512, 128
FLOPS = 2 * E * C * (K * H + K * N + H * N)

F32 = mybir.dt.float32
BF16 = mybir.dt.bfloat16
I32 = mybir.dt.int32
U32 = mybir.dt.uint32
U16 = mybir.dt.uint16
U8 = mybir.dt.uint8
FP8X4 = mybir.dt.float8_e4m3fn_x4
FP4X4 = mybir.dt.float4_e2m1fn_x4
RELU = mybir.ActivationFunctionType.Relu
COPY = mybir.ActivationFunctionType.Copy
ALU = mybir.AluOpType

P = 128
PACK = 4
PASS_ROWS = P * PACK
PASSES = K // PASS_ROWS
LAST = E - 1
HALF = C // 2
QUAD = 32
QUAD_ROWS = 4
LIST_ROWS = 16
PAIR = 2 * C
SPARE = 192
RING = 7
SCALAR_ALONE = 7
VECTOR_SHARE = 68
LAST_SHARE = 24
WORDS_AT = 4
ALIGN = 256
TAIL = 128


def tile_moe_elr_relu_kernel(
    tc, x_words, x_scales, w_words, w_scales, wa, wb, gate, offs, pos1, pos2, out
):
    nc = tc.nc
    with ExitStack() as ctx:
        keep = ctx.enter_context(tc.tile_pool(name="keep", bufs=1))
        ring = ctx.enter_context(tc.tile_pool(name="ring", bufs=RING))
        psum = ctx.enter_context(tc.psum_pool(name="psum", bufs=1))

        def kept(shape, dtype, name):
            return keep.tile(shape, dtype, name=name, align_bytes=ALIGN)

        def half(u):
            return slice(u * HALF, (u + 1) * HALF)

        def bank_name(e, u):
            return "bank%d_%d" % (e, u)

        offs_sb = keep.tile([P, E * C // LIST_ROWS], U16, name="offs_sb", align_bytes=ALIGN)
        pos_sb = [keep.tile([P, T // LIST_ROWS], U16, name="pos%d_sb" % r, align_bytes=ALIGN) for r in range(2)]
        xw_first = kept([P, (PASSES - 1) * T + SPARE], I32, "xw_first")
        xw_later = kept([P, T + SPARE], I32, "xw_later")
        xs = kept([P, PASSES * T + SPARE], U8, "xs")
        ws = kept([P, E * PASSES, N], U8, "ws")
        y_sb = kept([P, E * C], F32, "y_sb")
        gate_sb = [kept([P, T], F32, "gate%d" % r) for r in range(2)]

        nc.vector.memset(xs[:].bitcast(I32), 0)
        nc.vector.memset(xw_first[:, (PASSES - 1) * T :], 0)
        nc.vector.memset(xw_later[:, T:], 0)
        nc.vector.memset(ws[:].rearrange("p a n -> p (a n)").bitcast(I32), 0)

        wa_raw, raw_name, wb_raw, ww = {}, {}, {}, {}
        wa_rows = wa.rearrange("e (s p j) c -> p (e s) (j c)", p=P, j=PACK)
        words = x_words.rearrange("s p t d -> p s (t d)").bitcast(I32)
        steps = [(e, s) for e in range(E) for s in range(PASSES)]

        def load_wa(group):
            first = steps.index(group[0])
            name = "wa_raw%d" % first
            raw = kept([P, len(group), PACK * H], F32, name)
            nc.sync.dma_start(out=raw[:], in_=wa_rows[:, first : first + len(group)])
            for i, step in enumerate(group):
                wa_raw[step] = raw[:, i]
                raw_name[step] = name

        def load_ws(r):
            rows = w_scales.bitcast(I32).rearrange("e s (q r) w -> r q (e s) w", r=QUAD_ROWS)
            nc.sync.dma_start(out=ws[r:P:QUAD, :, :].bitcast(I32), in_=rows[r])

        def load_wb(lo, hi):
            raw = kept([P, hi - lo, PACK * N], F32, "wb_raw%d" % lo)
            nc.sync.dma_start(out=raw[:], in_=wb[lo:hi].rearrange("e (p j) c -> p e (j c)", j=PACK))
            for e in range(lo, hi):
                wb_raw[e] = raw[:, e - lo]

        def load_ww(lo, hi):
            fp4 = kept([P, (hi - lo) * PASSES, 2 * N], U8, "ww%d" % lo)
            rows = w_words.bitcast(I32).rearrange("e s p w -> p (e s) w")
            nc.sync.dma_start(out=fp4[:].bitcast(I32), in_=rows[:, lo * PASSES : hi * PASSES])
            for e in range(lo, hi):
                for s in range(PASSES):
                    ww[e, s] = fp4[:, (e - lo) * PASSES + s]

        nc.sync.dma_start(
            out=xw_first[:, : (PASSES - 1) * T].rearrange("p (s t) -> p s t", t=T), in_=words[:, : PASSES - 1]
        )
        nc.sync.dma_start(offs_sb[:], offs)
        load_wa(steps[0:1])
        scale_rows = x_scales.bitcast(I32).rearrange("s (q r) w -> r q s w", r=QUAD_ROWS)
        for r in range(QUAD_ROWS):
            queue = nc.scalar if r % 2 == 0 else nc.sync
            queue.dma_start(
                out=xs[r:P:QUAD, : PASSES * T].bitcast(I32).rearrange("p (s w) -> p s w", s=PASSES), in_=scale_rows[r]
            )
        for i in range(1, WORDS_AT):
            load_wa(steps[i : i + 1])
        nc.sync.dma_start(out=xw_later[:, :T], in_=words[:, PASSES - 1])

        xg, xsg = {}, {}
        pairs = range(E * C // PAIR)
        pair_list = [offs_sb[:, b * (PAIR // LIST_ROWS) : (b + 1) * (PAIR // LIST_ROWS)] for b in pairs]

        def gather_words(b, s, name):
            window = xw_later[:] if s == PASSES - 1 else xw_first[:, s * T : (s + 1) * T + SPARE]
            gathered = kept([P, PAIR], U32, name)
            nc.vector.tensor_copy(gathered[:], window.bitcast(U32).indirect(pair_list[b]))
            for i in range(2):
                xg[2 * b + i, s] = gathered[:, i * C : (i + 1) * C]

        for b in pairs:
            gather_words(b, 0, "xg%d_0" % b)

        def gather_bytes(b, s, name):
            gathered = kept([P, PAIR], U8, name)
            nc.vector.tensor_copy(gathered[:], xs[:, s * T : (s + 1) * T + SPARE].indirect(pair_list[b]))
            for i in range(2):
                xsg[2 * b + i, s] = gathered[:, i * C : (i + 1) * C]

        for b in pairs:
            for s in range(PASSES):
                gather_bytes(b, s, "xsg%d_%d" % (b, s))

        for i in range(WORDS_AT, E * PASSES):
            load_wa(steps[i : i + 1])
        for e in range(2):
            load_wb(e, e + 1)
        for r in range(QUAD_ROWS):
            load_ws(r)
        load_ww(0, 2)
        for e in range(2, E):
            load_wb(e, e + 1)
            load_ww(e, e + 1)
        for r, pos in enumerate((pos1, pos2)):
            nc.sync.dma_start(pos_sb[r][:], pos)
        for r in range(2):
            nc.sync.dma_start(out=gate_sb[r][:], in_=gate[r])

        h_ps = {}
        wb_codes, wb_scales, h_codes, h_scales = {}, {}, {}, {}

        def round_wa(step):
            rounded = ring.tile([P, PACK * H], BF16, name="wa_bf", align_bytes=ALIGN)
            dst = rounded[:].rearrange("p (g v m j) -> p g m j v", g=2, v=2, j=PACK)
            src = wa_raw[step].rearrange("p (j m g v) -> p g m j v", g=2, v=2, j=PACK)
            if steps.index(step) < SCALAR_ALONE:
                nc.scalar.copy(out=dst, in_=src)
            elif step == steps[-1]:
                nc.vector.tensor_copy(out=dst[:, 0], in_=src[:, 0])
                nc.vector.tensor_copy(out=dst[:, 1, :LAST_SHARE], in_=src[:, 1, :LAST_SHARE])
                nc.scalar.copy(out=dst[:, 1, LAST_SHARE:], in_=src[:, 1, LAST_SHARE:])
            else:
                nc.vector.tensor_copy(out=dst[:, :, :VECTOR_SHARE], in_=src[:, :, :VECTOR_SHARE])
                nc.scalar.copy(out=dst[:, :, VECTOR_SHARE:], in_=src[:, :, VECTOR_SHARE:])
            return rounded

        def mm_wa(e, s, codes, scales, outputs):
            for u in (1, 0):
                if s == 0:
                    h_ps[e, u] = psum.tile([P, PACK, HALF], F32, name=bank_name(e, u))
                for t in outputs:
                    m = slice(t * P, (t + 1) * P)
                    nc.tensor.matmul_mx(
                        out=h_ps[e, u][:, t, :],
                        lhsT=codes[:, m].bitcast(FP8X4), lhsT_scale=scales[:, m],
                        rhs=xg[e, s][:, half(u)].bitcast(FP8X4),
                        rhs_scale=xsg[e, s][:, half(u)],
                        start=(s == 0 and t == 0), stop=(s == PASSES - 1 and t == PACK - 1),
                    )

        def step_wa(e, s):
            rounded = round_wa((e, s))
            if (e, s) == steps[-1]:
                codes = kept([P, H], U32, "last_codes")
                scales = kept([P, H], U8, "last_scales")
            else:
                codes = ring.tile([P, H], U32, name="wa_codes", align_bytes=ALIGN)
                scales = ring.tile([P, H], U8, name="wa_scales", align_bytes=ALIGN)
            pieces = 2 if (e, s) == steps[-1] else 1
            width = H // pieces
            for g in range(pieces):
                cols = slice(g * width, (g + 1) * width)
                nc.vector.quantize_mx(
                    out=codes[:, cols].bitcast(FP8X4), scales=scales[:, cols],
                    in_=rounded[:, g * PACK * width : (g + 1) * PACK * width],
                )
                mm_wa(e, s, codes, scales, range(g * PACK // pieces, (g + 1) * PACK // pieces))

        def round_wb(e, rounded):
            dst = rounded.rearrange("p (c n j) -> p c j n", n=4, j=PACK)
            src = wb_raw[e].rearrange("p (j c n) -> p c j n", n=4, j=PACK)
            if e % 2 == 1:
                nc.vector.tensor_copy(out=dst, in_=src)
            else:
                nc.scalar.copy(out=dst, in_=src)

        def quantise_wb(lo, hi, rounded):
            codes = kept([P, (hi - lo) * N], U32, "wb_codes%d" % lo)
            scales = kept([P, (hi - lo) * N], U8, "wb_scales%d" % lo)
            nc.vector.quantize_mx(out=codes[:].bitcast(FP8X4), scales=scales[:], in_=rounded)
            for e in range(lo, hi):
                wb_codes[e] = codes[:, (e - lo) * N : (e - lo + 1) * N]
                wb_scales[e] = scales[:, (e - lo) * N : (e - lo + 1) * N]

        def hidden(e, name):
            rounded = kept([P, C, PACK], BF16, name)
            h_codes[e] = kept([P, C], U32, "h_codes%d" % e)
            h_scales[e] = kept([P, C], U8, "h_scales%d" % e)
            by_slot = [h_ps[e, u][:].rearrange("p t n -> p n t") for u in range(2)]
            nc.scalar.activation(out=rounded[:, half(0), :], in_=by_slot[0], func=RELU)
            quarters = [slice(0, HALF // 2), slice(HALF // 2, HALF)] if e == LAST else [slice(0, HALF)]
            for part in quarters:
                nc.vector.tensor_scalar_max(
                    out=rounded[:, HALF + part.start : HALF + part.stop, :], in0=by_slot[1][:, part, :], scalar1=0.0
                )
            pieces = [slice(HALF, HALF + HALF // 2), half(0), slice(HALF + HALF // 2, C)] if e == LAST else [slice(0, C)]
            for cols in pieces:
                nc.vector.quantize_mx(
                    out=h_codes[e][:, cols].bitcast(FP8X4), scales=h_scales[e][:, cols],
                    in_=rounded[:, cols, :].rearrange("p n t -> p (n t)"),
                )

        def mm_w(e, cols, target, opens):
            for s in range(PASSES):
                nc.tensor.matmul_mx(
                    out=target,
                    lhsT=ww[e, s].bitcast(FP4X4), lhsT_scale=ws[:, e * PASSES + s, :],
                    rhs=xg[e, s][:, cols].bitcast(FP8X4), rhs_scale=xsg[e, s][:, cols],
                    start=(opens and s == 0), stop=(not opens and s == PASSES - 1),
                )

        def mm_wb(e, target, cols, opens):
            nc.tensor.matmul_mx(
                out=target,
                lhsT=wb_codes[e].bitcast(FP8X4), lhsT_scale=wb_scales[e],
                rhs=h_codes[e][:, cols].bitcast(FP8X4), rhs_scale=h_scales[e][:, cols],
                start=opens, stop=not opens,
            )

        whole = slice(0, C)
        relu_after = {(1, 2): 0, (2, 1): 1, (3, 0): 2}
        y_ps = {}

        def open_y(e):
            y_ps[e] = psum.tile([P, C], F32, name=bank_name(e, 0))
            mm_w(e, whole, y_ps[e][:], True)

        def close_y(e):
            mm_wb(e, y_ps[e][:], whole, False)
            nc.scalar.copy(out=y_sb[:, e * C : (e + 1) * C], in_=y_ps[e][:])

        for i, (e, s) in enumerate(steps):
            step_wa(e, s)
            if i == 0:
                for later in range(1, PASSES):
                    gather_words(0, later, "xg0_%d" % later)
            if i in (3, 4):
                gather_words(1, i - 2, raw_name[e, s])
            if (e, s) in relu_after:
                hidden(relu_after[e, s], raw_name[e, s])

        early = kept([P, 2 * PACK * N], BF16, raw_name[steps[-1]])
        for e in range(2):
            round_wb(e, early[:, e * PACK * N : (e + 1) * PACK * N])
        for e in range(2):
            quantise_wb(e, e + 1, early[:, e * PACK * N : (e + 1) * PACK * N])
        hidden(LAST, "wb_raw1")
        late = {e: kept([P, PACK * N], BF16, name) for e, name in ((LAST - 1, "last_codes"), (LAST, "last_scales"))}
        for e in late:
            round_wb(e, late[e][:])
        for e in late:
            quantise_wb(e, e + 1, late[e][:])
        for e in range(2):
            open_y(e)
            close_y(e)
        open_y(LAST - 1)
        y_last = [psum.tile([P, HALF], F32, name=bank_name(u, 1)) for u in range(2)]
        for u in (1, 0):
            mm_w(LAST, half(u), y_last[u][:], True)
        close_y(LAST - 1)
        for u in (1, 0):
            mm_wb(LAST, y_last[u][:], half(u), False)
        nc.vector.tensor_copy(out=y_sb[:, LAST * C + HALF :], in_=y_last[1][:])
        nc.scalar.copy(out=y_sb[:, LAST * C : LAST * C + HALF], in_=y_last[0][:])

        first = kept([P, T], F32, "first")
        second = [kept([P, T // 2], F32, "second%d" % b) for b in range(2)]
        second_gated = kept([P, T], F32, "second_gated")
        res = kept([P, T], F32, "res")

        def entries(r, span):
            return pos_sb[r][:, span.start // LIST_ROWS : span.stop // LIST_ROWS]

        halves = [slice(0, T // 2), slice(T // 2, T)]
        for b, span in enumerate(halves):
            nc.scalar.activation(second[b][:], y_sb[:].indirect(entries(1, span)), COPY)
        nc.vector.tensor_tensor(first[:], y_sb[:].indirect(pos_sb[0][:]), gate_sb[0][:], ALU.mult)
        for b, span in enumerate(halves):
            nc.vector.tensor_tensor(second_gated[:, span], second[b][:], gate_sb[1][:, span], ALU.mult)
        for span in (slice(0, T - 2 * TAIL), slice(T - 2 * TAIL, T - TAIL), slice(T - TAIL, T)):
            nc.vector.tensor_tensor(res[:, span], first[:, span], second_gated[:, span], ALU.add)
            nc.sync.dma_start(out=out[:, span], in_=res[:, span])
